import numpy as np, ml_dtypes
CORES = [6,15,38,47]
N = 4
BF = ml_dtypes.bfloat16
def gentries(a):
    return np.ascontiguousarray(a.reshape(8, 16, -1).transpose(0, 2, 1)).reshape(8, -1)
def gtable(e):
    e = np.asarray(e); return np.ascontiguousarray(e.reshape(8, -1, 16).transpose(0, 2, 1)).reshape(128, -1).astype(np.int32)
V, P, XC, B, RO = 256, 256, 4096, 1, 4
E = 16 * V
def place_record(n, a, p, t):
    return ((n * (2 * a + 1) >> 4) + n + 37 * p + 77 * t) & (XC - 1)
def seat(rng, ln, key=None, mix=True, pair=False):
    oc = np.full((N, 8, E), P, np.int64); qs = np.full((N, 8, 16 * P), E, np.int64)
    for r in range(N):
        for g in range(8):
            at = np.flatnonzero((np.arange(16) < ln[r, g][:, None]).reshape(-1))
            if pair and g & 1: at = at[np.argsort(2 * np.minimum(at, at ^ (16 * B)) + (at > (at ^ (16 * B))))]
            s = rng.permutation(16 * P) if key is None else np.argsort(key[r, g].reshape(-1))
            s = s[:len(at)]
            if mix: s = rng.permutation(s)
            oc[r, g, at] = s >> 4; qs[r, g, s] = at
    return oc, qs
def put(oc, qs, r, g, s, n):
    b = int(np.flatnonzero(qs[r, g] == n)[0]); m = int(qs[r, g, s])
    qs[r, g, s] = n; qs[r, g, b] = m; oc[r, g, m] = b >> 4; oc[r, g, n] = s >> 4
def aim(w, y, u):
    i = np.arange(1, 16)[:, None]
    w[0] = (u - np.sum(16 * i * w[1:] + np.minimum(w[1:], y[1:, None]), axis=0)) & (V - 1)
def pack(x, want, oc, qs, th):
    return {"x": np.ascontiguousarray(x.reshape(N, 128, XC)).astype(np.float32).astype(BF), "want": np.stack([want.reshape(128, P)] * N).astype(np.float32).astype(BF),
            "oc": np.stack([gtable(a) for a in oc]), "qs": np.stack([gtable(a) for a in qs]), "th": np.repeat(th, 16, axis=1).reshape(N, 128, 1).astype(np.int32)}
def goods(rng):
    return rng.integers(0, 256, (N, 8, 16, XC)), rng.integers(0, 256, (8, 16, P))
def setup_inputs(rng):
    x, want = goods(rng); oc, qs = seat(rng, rng.integers(8, 17, (N, 8, V)))
    return pack(x, want, oc, qs, rng.integers(450, 901, (N, 8)))
def setup_inputs_alike(rng):
    x, want = goods(rng); ln = rng.choice(np.array([16, 16, 8, 3, 12]), (N, 8, V))
    ln[:, 2] = 16; ln[:, 4] = rng.integers(12, 16, (N, V)); ln[:, 6] = rng.integers(12, 16, (N, V)); ln[:, 6, 1] = 16; ln[N - 1, 6, V - 1] = 15
    key = rng.random((N, 8, P, 1)) + 0.0001 * rng.random((N, 8, P, 16))
    oc, qs = seat(rng, ln, key, False, True)
    want[3] = want[3][:, :1]; x[N - 1, 5] = x[N - 1, 5] >> 1
    key = rng.random((N, 8, P, 16)); one = np.arange(16) == rng.integers(0, 16, (N, P, 1))
    key[:, 4] = np.where(one, -1, np.where(np.roll(one, 1, axis=2), 9, key[:, 4]))
    key[:, 6, 1:N + 1] = 9; key[:, 6, P - 1] = 9; key[N - 1, 6, P - 1, :15] = -1
    for r in range(N): key[r, 6, r + 1, r] = -1
    oc2, qs2 = seat(rng, ln, key)
    oc[:, 2:7:2] = oc2[:, 2:7:2]; qs[:, 2:7:2] = qs2[:, 2:7:2]
    n = np.arange(E); m = n ^ (16 * B)
    for r in range(N):
        a = np.where((n & 15) == 0, n >> 4, np.roll(oc[r, 2], 1)); c = place_record(m, a[m], oc[r, 2], 0)
        y = x[r, 2] >> 1; y[:, c] = y[:, c] | 128; x[r, 2] = y
        put(oc, qs, r, 6, 16 * (r + 1) + r, 128)
    for k in range(15): put(oc, qs, N - 1, 6, 16 * (P - 1) + k, E - 16 + k)
    y = rng.integers(0, 256, 16); y[0] = 255; x[:, 4] = y[:, None]; want[4] = want[4][:, :1]; aim(want[4], y, 0)
    u = 2 + rng.integers(0, V - 3, P); u[1:N + 1] = 1; u[P - 1] = V - 1
    x[:, 6] = 255; aim(want[6], np.full(16, 255), u)
    th = rng.integers(600, 1500, (N, 8)); th[:, 2] = 4080
    return pack(x, want, oc, qs, th)
def setup_inputs_ties(rng):
    x, want = goods(rng); x = 85 * (x >> 6); want = 85 * (want >> 6)
    oc, qs = seat(rng, rng.integers(8, 17, (N, 8, V)))
    for a in (x, oc, qs): a[:, ::2] = a[:1, ::2]
    x[0, 2] = np.minimum(x[0, 2], 170); x[0, 6] = np.minimum(x[0, 6], 170)
    return pack(x, want, oc, qs, 85 * rng.integers(4, 11, (N, 8)) - rng.integers(0, 2, (N, 8)))
def setup_inputs_corners(rng):
    x, want = goods(rng); ln = rng.choice(np.array([0, 1, 15, 16]), (N, 8, V))
    kind = rng.random((N, 8, 1, XC)); x = np.where(kind < 0.4, 255, np.where(kind < 0.5, 0, x))
    cls = rng.integers(0, 4, (8, 1, P)); kind = rng.random((8, 1, P)); many = np.full((8, 16, P), 255); many[:, 1:2] = 255 - cls
    want = np.where(kind < 0.6, many, np.where(kind < 0.7, 0, want))
    want[7, :, ::16] = 255; want[7, 7, ::16] = 254
    for g in range(8):
        x[:g % N, g, 0] = np.minimum(x[:g % N, g, 0], 254)
        for c in range(4): ln[:, g, (16 * 120 * 255 + 4080 - 17 * c) & (V - 1)] = (15, 0, 16, 1)[(g + c) & 3]
    ln[:, 7, V - 1] = 15; ln[:, 0, V - 1] = 16; ln[:, 7, 0] = 16
    c = rng.integers(0, 5, (N, 8, P, 1)); c[:, :, 4::9] = 3
    one = np.arange(16) == rng.integers(0, 16, (N, 8, P, 1))
    key = rng.random((N, 8, P, 1)) + 0.0001 * rng.random((N, 8, P, 16))
    key = key + np.where(c == 0, 0, np.where(c == 1, np.where(one, 3, 0), np.where(c == 2, np.where(one, -3, 3), np.where(c == 3, 6, 1))))
    key[N - 1, 7, 0] = np.where(np.arange(16) < 15, -1, 9)
    oc, qs = seat(rng, ln, key)
    th = rng.choice(np.array([0, 1, 1000, 2000, 4080]), (N, 8)); th[:, ::2] = 4080; th[:, 5] = 4079; th[:, 7] = 4080
    return pack(x, want, oc, qs, th)
def setup_inputs_ends(rng):
    v = np.arange(V); low = np.minimum(v, v ^ B)
    ln = np.where((rng.random((N, 8, V)) < 0.35)[..., low], 16, 0)
    for q in (0, V - 1): ln[..., q] = 16; ln[..., q ^ B] = 16
    who = rng.random((N, 8, P, 1)); who[:, :, 0] = -1; who[:, :, P - 1] = -1
    oc, qs = seat(rng, ln, who + 0.0001 * rng.random((N, 8, P, 16)))
    kind = rng.random((8, 1, P)); want = np.where(kind < 0.25, 255, np.where(kind < 0.4, 0, 255 * rng.integers(0, 2, (8, 16, P))))
    want[:, :, 0] = 255; want[:, :, P - 1] = 255; want[:, :, P // 2] = 0; want[:, :, P - 2] = 0
    kind = rng.random((N, 8, 1, XC)); x = np.where(kind < 0.3, 255, np.where(kind < 0.45, 0, 255 * rng.integers(0, 2, (N, 8, 16, XC))))
    x[..., 0] = 255; x[..., XC - 1] = 255
    for r in range(N):
        for g in range(8):
            put(oc, qs, r, g, 16 * P - 1, E - 1); put(oc, qs, r, g, 0, 0)
            x[r, g, :, int(place_record(E - 1, int(oc[r, g, E - 2]), P - 1, 0))] = 255
    th = np.where(rng.random((N, 8)) < 0.3, 0, 4080); th[:, 0] = 4080; th[:, 1] = 0; th[:, 7] = 4080
    return pack(x, want, oc, qs, th)
def setup_inputs_spread(rng):
    x = np.minimum((np.exp2(8 * rng.random((N, 8, 1, XC))) * rng.random((N, 8, 16, XC))).astype(np.int64), 255)
    want = np.minimum((np.exp2(2 + 6 * rng.random((8, 1, P))) * rng.random((8, 16, P))).astype(np.int64), 255)
    ln = np.minimum((17 * rng.random((N, 8, V)) ** rng.choice(np.array([0.3, 0.6, 1.0, 2.0]), (N, 8, 1))).astype(np.int64), 16)
    oc, qs = seat(rng, ln)
    return pack(x, want, oc, qs, np.minimum(np.exp2(12 * rng.random((N, 8))).astype(np.int64), 4080))
def check_inputs(d):
    bad = []
    for k, hi in (("x", 255), ("want", 255), ("oc", P), ("qs", E), ("th", 4080)):
        a = np.asarray(d[k]).astype(np.float64)
        if not np.all((a >= 0) & (a <= hi)): bad.append("range of " + k)
        elif not np.all(a == np.floor(a)): bad.append("whole numbers of " + k)
    w = np.asarray(d["want"]).astype(np.float32)
    if not np.all(w == w[:1]): bad.append("want alike on all ranks")
    t = np.asarray(d["th"]).reshape(N, 8, 16)
    if not np.all(t == t[:, :, :1]): bad.append("th alike in the rows of a group")
    if "range of oc" in bad or "range of qs" in bad: return bad
    o = np.stack([gentries(a) for a in d["oc"]]).astype(np.int64); q = np.stack([gentries(a) for a in d["qs"]]).astype(np.int64)
    b = (o < P).reshape(N, 8, V, 16)
    if np.any(b[..., 1:] & ~b[..., :-1]): bad.append("queues of oc without gaps")
    ok = True; person = np.arange(16 * P) >> 4
    for r in range(N):
        for g in range(8):
            n = np.bincount(q[r, g], minlength=E + 1)[:E]; back = np.full(E + 1, P, np.int64); back[q[r, g]] = person
            ok = ok and np.array_equal(n, (o[r, g] < P).astype(n.dtype)) and np.array_equal(back[:E], o[r, g])
    if not ok: bad.append("every occupied place of oc in just one slot of qs, of its person")
    return bad
def reference(x, want, oc, qs, th):
    xs = x.astype(np.float32).astype(np.int32).reshape(N, 8, 16, XC); ws = want.astype(np.float32).astype(np.int32).reshape(N, 8, 16, P)
    wp = np.concatenate([ws, np.zeros((N, 8, 16, 1), np.int32)], axis=3); wsum = np.add.reduce(16 * np.arange(16)[:, None] * ws.astype(np.int64), axis=2)
    o = np.stack([gentries(a) for a in oc]).astype(np.int64)
    q = np.stack([gentries(a) for a in qs]).astype(np.int64)
    lim = th.astype(np.int64).reshape(N, 8, 16)[:, :, :1]
    n = np.arange(E); mate = n ^ (16 * B); v = n >> 4; head = (n & 15) == 0; none = np.full((N, 8, 1), E, np.int64)
    for t in range(RO):
        occ = o < P; ahead = np.where(head, v, np.roll(o, 1, axis=2))
        w = np.take_along_axis(wp, o[:, :, None, :], 3)
        own = np.add.reduce(np.minimum(np.take_along_axis(xs, place_record(n, ahead, o, t)[:, :, None, :], 3), w), axis=2).astype(np.int64)
        other = np.add.reduce(np.minimum(np.take_along_axis(xs, place_record(mate, ahead[..., mate], o, t)[:, :, None, :], 3), w), axis=2).astype(np.int64)
        swap = occ & occ[..., mate] & (other + other[..., mate] > own + own[..., mate])
        o2 = np.where(swap, o[..., mate], o); c = np.where(swap, other[..., mate], own)
        qd = np.take_along_axis(np.concatenate([np.where(swap, mate, n), none], axis=2), q, 2)
        best = np.max(np.take_along_axis(np.concatenate([c, np.full((N, 8, 1), -1, np.int64)], axis=2), qd, 2).reshape(N, 8, P, 16), axis=3)
        top = np.max(best, axis=0); holder = np.argmax(best, axis=0)
        tp = np.concatenate([np.broadcast_to(top, (N, 8, P)), np.zeros((N, 8, 1), np.int64)], axis=2)
        go = (c < np.take_along_axis(tp, o2, 2) - lim) | (head & ((v & 7) == t))
        stay = (occ & ~go).astype(np.int64).reshape(N, 8, V, 16)
        to = np.where(stay == 1, 16 * np.arange(V)[:, None] + np.add.accumulate(stay, axis=3) - stay, E).reshape(N, 8, E)
        o = np.full((N, 8, E + 1), P, np.int64); np.put_along_axis(o, to, o2, 2); o = np.ascontiguousarray(o[..., :E])
        q = np.take_along_axis(np.concatenate([to, none], axis=2), qd, 2)
        ln = np.add.reduce(stay, axis=3); empty = q.reshape(N, 8, P, 16) == E; u = (wsum + top) & (V - 1)
        for r in range(N):
            for g in range(8):
                p = np.flatnonzero(np.any(empty[r, g], axis=1) & (top[g] >= 0) & (holder[g] == r)); p = p[ln[r, g, u[r, g, p]] < 16]
                k, i = np.unique(u[r, g, p], return_index=True); p = p[i]; at = 16 * k + ln[r, g, k]
                o[r, g, at] = p; q[r, g, 16 * p + np.argmax(empty[r, g, p], axis=1)] = at
    return {"yoc": np.stack([gtable(a) for a in o]).astype(np.float32), "yq": np.stack([gtable(a) for a in q]).astype(np.float32)}

@@ -1,0 +1,533 @@
+from concourse.bass import DstId, RemoteDMATransfer
+from concourse.mybir import AluOpType, AxisListType, ActivationFunctionType
+
+A = AluOpType
+F = ActivationFunctionType
+RO = 4
+NOB = -29952.0
+
+SCRATCH = {}
+for _n, _w, _d in [
+    ("xs", 4096, "bfloat16"), ("ww", 272, "bfloat16"), ("wg", 4096, "bfloat16"), ("mn", 8192, "bfloat16"),
+    ("cw", 4112, "bfloat16"), ("cg", 4096, "bfloat16"), ("xw", 4112, "bfloat16"), ("xg", 4096, "bfloat16"),
+    ("mw", 272, "bfloat16"), ("mg", 4096, "bfloat16"), ("lw", 256, "bfloat16"), ("lg", 256, "bfloat16"),
+    ("qw", 512, "bfloat16"),
+    ("roc", 256, "int32"), ("rqs", 256, "int32"), ("rth", 1, "int32"),
+    ("zs", 144, "bfloat16"), ("za", 144, "bfloat16"), ("zf", 144, "bfloat16"), ("zw", 144, "bfloat16"),
+    ("br", 2048, "float16"), ("bm", 128, "float32"), ("e0", 160, "float32"), ("e1", 160, "float32"),
+    ("idb", 128, "bfloat16"),
+    ("ip", 1, "int32"), ("ki", 1, "int32"), ("gi", 1, "int32"), ("cf", 16, "float32"), ("keq", 16, "float32"),
+    ("ci", 256, "float32"), ("c16", 16, "float32"), ("cm", 128, "float32"), ("nlf", 256, "float32"), ("ni", 256, "int32"),
+    ("na", 256, "int32"), ("thl", 1024, "float32"), ("jl", 256, "float32"), ("rr", 256, "float32"),
+    ("pfr", 256, "float32"), ("pfl", 16, "float32"), ("pll", 16, "float32"), ("pv", 256, "bfloat16"), ("ws", 16, "float32"),
+    ("hv", 16, "float32"), ("tf", 256, "float32"), ("tg", 256, "float32"), ("rt", 256, "float32"), ("of", 256, "float32"),
+    ("ou", 256, "uint16"), ("ou2", 256, "uint16"),
+    ("qi", 256, "int32"), ("qd", 256, "int32"), ("qu", 256, "uint16"), ("qdu", 256, "uint16"), ("dq", 256, "float32"), ("qa", 256, "int32"),
+    ("a2", 256, "float32"), ("t1", 256, "int32"), ("t2", 256, "int32"), ("hj", 512, "int32"),
+    ("hu", 512, "uint16"), ("em", 256, "bfloat16"),
+    ("chi", 256, "bfloat16"), ("clo", 256, "bfloat16"), ("cs", 256, "float32"), ("cx", 256, "float32"),
+    ("g32", 256, "float32"), ("hq", 256, "int32"),
+    ("mm", 16, "float32"), ("m16", 16, "float16"), ("mt", 256, "bfloat16"), ("lm", 16, "float32"), ("h1", 16, "float32"), ("h2", 16, "float32"),
+    ("s1", 16, "int32"), ("ui", 16, "int32"), ("a16", 256, "float32"), ("a17", 256, "float32"), ("f16", 16, "float32"),
+    ("va", 16, "float32"), ("vb", 16, "float32"), ("uc", 16, "float32"), ("uh", 16, "float16"), ("kr", 256, "float32"),
+    ("tk", 1024, "float32"), ("res", 16, "float32"), ("wi", 16, "float32"), ("uo", 16, "float32"), ("uou", 16, "uint16"), ("uu", 16, "uint16"),
+    ("lv", 256, "float32"), ("st", 256, "float32"), ("lvb", 256, "bfloat16"), ("xl", 256, "bfloat16"), ("le", 16, "bfloat16"),
+    ("ap", 64, "float32"), ("sl", 64, "float32"), ("land", 256, "float32"), ("bs", 64, "float32"),
+]:
+    SCRATCH[_n] = ("sbuf", [128, _w], _d)
+for _n, _r, _w, _d in [
+    ("yb", 16, 17, "int32"), ("tb", 16, 17, "int32"), ("tr", 8, 32, "float32"), ("oi", 8, 32, "int32"), ("o2", 8, 32, "int32"),
+    ("hi", 16, 32, "int32"), ("p37", 8, 32, "float32"), ("m1s", 8, 32, "float32"), ("sw", 8, 32, "bfloat16"), ("ccs", 8, 32, "float32"),
+    ("e1l", 8, 32, "float32"), ("c2l", 8, 32, "float32"), ("dob", 8, 16, "float32"), ("ds", 8, 16, "float32"),
+    ("t8", 16, 8, "float32"), ("t8b", 16, 8, "float32"), ("t4", 16, 4, "float32"), ("t2x", 16, 2, "float32"), ("jv", 16, 16, "float32"),
+]:
+    SCRATCH[_n] = ("sbuf", [128, _r, _w], _d)
+for _n in ("p1", "p3", "p4", "p5", "p6"):
+    SCRATCH[_n] = ("psum", [128, 512], "float32")
+SCRATCH["p0"] = ("psum", [128, 32, 16], "float32")
+SCRATCH["p2"] = ("psum", [128, 16, 32], "float32")
+SCRATCH["p7"] = ("psum", [128, 16, 32], "float32")
+SEMAPHORES = ["sv", "ss", "st", "sg", "snt", "arr0", "arr1", "arr2", "arr3", "dx", "dw", "doc", "dqs", "dth",
+              "dhi", "dlo", "dsw", "dxl", "dle", "dyo", "dyq"]
+QSEM = {"v": "sv", "s": "ss", "t": "st", "g": "sg"}
+
+
+def rank_program(g, core, T, topo):
+    rank = T.rank_of(core)
+    if rank is None:
+        return
+    n_ranks = len(T.cores)
+    queues = {"v": g.vector, "s": g.scalar, "t": g.tensor, "y": g.sync, "g": g}
+    cnt = dict((s, 0) for s in SEMAPHORES)
+    known = dict((q, {}) for q in queues)
+    log = dict((n, []) for n in SCRATCH)
+    psum = set(n for n in SCRATCH if SCRATCH[n][0] == "psum")
+
+    def c(name, a=0, b=None, step=1):
+        shp = SCRATCH[name][1]
+        if len(shp) == 3:
+            w = shp[2]
+            if b is None:
+                b = shp[1] * w
+            return (T[name][:, a // w:b // w, :], name, a, b)
+        if b is None:
+            b = shp[1]
+        return (T[name][:, a:b:step] if step > 1 else T[name][:, a:b], name, a, b)
+
+    def k3(name, lo, hi, r0=0, r1=None):
+        shp = SCRATCH[name][1]
+        if r1 is None:
+            r1 = shp[1]
+        return (T[name][:, r0:r1, lo:hi], name, r0 * shp[2], r1 * shp[2])
+
+    def k1(name, j):
+        shp = SCRATCH[name][1]
+        return (T[name][:, :, j], name, 0, shp[1] * shp[2])
+
+    def pr(name, par, r0=0):
+        return k3(name, 16 * par, 16 * par + 16, r0, r0 + 8)
+
+    def order(q, rd, wr):
+        need = {}
+        for acc, isw in [(r, False) for r in rd] + [(w, True) for w in wr]:
+            _, name, lo, hi = acc
+            for (l2, h2, w2, q2, sem, val) in log[name]:
+                if (name in psum and q2 != q) or (l2 < hi and lo < h2 and (isw or w2)):
+                    if need.get(sem, 0) < val:
+                        need[sem] = val
+        for sem in sorted(need):
+            if known[q].get(sem, 0) < need[sem]:
+                queues[q].wait_ge(T.sem[sem], need[sem])
+                known[q][sem] = need[sem]
+
+    def note(q, rd, wr, sem, val):
+        for (_, name, lo, hi) in rd:
+            log[name] = [e for e in log[name] if not (e[3] == q and e[4] == sem and not e[2] and lo <= e[0] and e[1] <= hi)]
+            log[name].append((lo, hi, False, q, sem, val))
+        for (_, name, lo, hi) in wr:
+            log[name] = [e for e in log[name] if not (lo <= e[0] and e[1] <= hi and (name not in psum or e[3] == q))]
+            log[name].append((lo, hi, True, q, sem, val))
+
+    def run(q, rd, wr, call):
+        order(q, rd, wr)
+        sem = QSEM[q]
+        cnt[sem] += 1
+        call(queues[q]).then_inc(T.sem[sem], 1)
+        note(q, rd, wr, sem, cnt[sem])
+
+    def cols(*xs):
+        return [x for x in xs if isinstance(x, tuple)]
+
+    def raw(x):
+        return x[0] if isinstance(x, tuple) else x
+
+    def tt(out, a, b, op):
+        run("v", [a, b], [out], lambda v: v.tensor_tensor(out[0], a[0], b[0], op))
+
+    def ts(out, a, s1, op0, s2=None, op1=None):
+        if op1 is None:
+            run("v", [a] + cols(s1), [out], lambda v: v.tensor_scalar(out[0], a[0], raw(s1), None, op0))
+        else:
+            run("v", [a] + cols(s1, s2), [out], lambda v: v.tensor_scalar(out[0], a[0], raw(s1), raw(s2), op0, op1))
+
+    def cp(out, a):
+        run("v", [a], [out], lambda v: v.tensor_copy(out[0], a[0]))
+
+    def fill(out, x):
+        run("v", [], [out], lambda v: v.memset(out[0], x))
+
+    def scan(out, d0, d1):
+        run("v", [d0, d1], [out], lambda v: v.tensor_tensor_scan(out[0], d0[0], d1[0], 0.0, A.mult, A.add))
+
+    def act(out, a, func=F.Copy, **kw):
+        k2 = dict((k, raw(kw[k])) for k in kw)
+        run("s", [a] + cols(*kw.values()), [out], lambda s: s.activation(out[0], a[0], func, **k2))
+
+    def gat(q, out, win, off):
+        if q == "v":
+            run("v", [win, off], [out], lambda v: v.tensor_copy(out[0], win[0].indirect(off[0])))
+        else:
+            run("s", [win, off], [out], lambda s: s.activation(out[0], win[0].indirect(off[0]), F.Copy))
+
+    def mms(items, out):
+        rd = []
+        for it in items:
+            rd += [it[1], it[2]]
+        order("t", rd, [out])
+        cnt["st"] += 1
+        for k, (o, l, r, a, b) in enumerate(items):
+            i = g.tensor.matmul(o[0], l[0], r[0], a, b)
+            if k == len(items) - 1:
+                i.then_inc(T.sem["st"], 1)
+        note("t", rd, [out], "st", cnt["st"])
+
+    def ext(out, z, name, c0, n):
+        mms([(out, c(z, 15 - i, 143 - i), c(name, 16 * c0 + i, 16 * (c0 + n), 16), i == 0, i == 15) for i in range(16)], out)
+
+    def dma(q, out, in_, sem):
+        rd = cols(in_)
+        wr = cols(out)
+        order(q, rd, wr)
+        cnt[sem] += 16
+        queues[q].dma_start(raw(out), raw(in_)).then_inc(T.sem[sem], 16)
+        note(q, rd, wr, sem, cnt[sem])
+
+    def lane(name, f, w):
+        return (T[name][f::16, 0:w], name, 0, w)
+
+    dma("y", c("roc"), T.oc[:, :], "doc")
+    dma("y", c("rqs"), T.qs[:, :], "dqs")
+    fill(c("ww"), 0.0)
+    dma("s", c("rth"), T.th[:, :], "dth")
+    dma("s", c("xs"), T.x[:, :], "dx")
+    dma("y", c("ww", 1, 257), T.want[:, :], "dw")
+
+    def iota(out, pattern, base, cm):
+        if SCRATCH[out[1]][2] == "int32":
+            run("g", [], [out], lambda e: e.iota(out[0], pattern, base, cm))
+        else:
+            run("g", [], [out], lambda e: e.iota(out[0], pattern, base, cm, allow_small_or_imprecise_dtypes=True))
+
+    def col(j):
+        return c("cf", j, j + 1)
+
+    iota(c("ip"), [[0, 1]], 0, 1)
+    iota(c("ci"), [[1, 256]], 0, 0)
+    iota(c("c16"), [[1, 16]], 0, 0)
+    iota(c("jl"), [[0, 16], [-1, 16]], 16, 0)
+    iota(c("cm"), [[16, 8], [0, 16]], 0, 0)
+    ts(c("ki"), c("ip"), 15, A.bitwise_and)
+    tt(c("gi"), c("ip"), c("ki"), A.subtract)
+    cp(col(0), c("ip"))
+    cp(col(1), c("ki"))
+    ts(col(2), c("gi"), 15.0, A.add)
+    ts(col(3), c("ip"), 16.0, A.add)
+    ts(col(4), c("ki"), 256.0, A.mult)
+    ts(col(5), c("ki"), 32.0, A.mult, 1.0, A.add)
+    cp(col(6), c("gi"))
+    ts(col(10), c("ki"), 16.0, A.mult)
+    ts(c("s1", 0, 1), c("ip"), 16, A.bitwise_and)
+    ts(col(8), c("s1", 0, 1), 1.0 / 16, A.mult)
+    ts(col(7), col(8), -1.0, A.mult, 1.0, A.add)
+    ts(c("keq"), c("c16"), col(1), A.is_equal)
+    tt(col(9), c("keq", 0, 1), c("keq", 1, 2), A.add)
+    ts(c("e0"), c("ci", 0, 160), col(3), A.is_equal, col(7), A.mult)
+    ts(c("e1"), c("ci", 0, 160), col(3), A.is_equal, col(8), A.mult)
+
+    def swap16(psname):
+        for de in range(2):
+            cp(c("rt", 128 * de, 128 * de + 128), pr("tr", de))
+        for al in range(2):
+            o = c(psname, 128 * al, 128 * al + 128)
+            mms([(o, c("e%d" % al, 16 + 16 * (al - de), 144 + 16 * (al - de)), c("rt", 128 * de, 128 * de + 128), de == 0, de == 1)
+                 for de in range(2)], o)
+        for al in range(2):
+            cp(pr("tr", al), c(psname, 128 * al, 128 * al + 128))
+
+    def flip(a):
+        return (T.tr[:, a, :], "tr", 32 * a, 32 * a + 32)
+
+    def conv_in(src, psname):
+        for a in range(8):
+            i, o = c(src, 32 * a, 32 * a + 32), flip(a)
+            run("v", [i], [o], lambda v: v.transpose(o[0], i[0]))
+        swap16(psname)
+
+    def conv_out(dst, psname):
+        swap16(psname)
+        for a in range(8):
+            o, i = c(dst, 32 * a, 32 * a + 32), flip(a)
+            run("v", [i], [o], lambda v: v.transpose(o[0], i[0]))
+
+    for q in range(16):
+        cp(c("tf", 16 * q, 16 * q + 16), c("roc", q, 256, 16))
+    conv_in("tf", "p1")
+    cp(c("of"), c("tr"))
+    ts(c("tg"), c("of"), 256.0, A.is_lt)
+    ts(c("of"), c("of"), 1.0, A.add)
+    tt(c("oi"), c("of"), c("tg"), A.mult)
+    ts(c("nlf"), c("ci"), col(4), A.add)
+    cp(c("p6", 0, 256), c("nlf"))
+    ts(c("hv"), c("c16"), 2.0, A.mult, col(5), A.add)
+    ts(c("zs"), c("ci", 0, 144), col(2), A.is_equal)
+    ts(c("idb"), c("ci", 0, 128), col(0), A.is_equal)
+
+    def q_lists():
+        cp(c("qu"), c("qi"))
+        ts(c("qa"), c("qi"), 16, A.bitwise_and)
+        ts(c("dq"), c("qa"), -2.0, A.mult, 16.0, A.add)
+
+    def more_constants():
+        ts(c("za"), c("ci", 0, 144), col(2), A.is_equal, col(9), A.mult)
+        ts(c("zf"), c("ci", 0, 144), col(2), A.is_equal, c("keq", 2, 3), A.mult)
+        ts(c("zw"), c("ci", 0, 144), col(2), A.is_equal, col(10), A.mult)
+        o = c("p5", 0, 16)
+        mms([(o, c("zw", 15 - i, 143 - i), c("ww", 1 + i, 257, 16), i == 0, i == 15) for i in range(16)], o)
+        cp(c("ws"), o)
+        for n in ("cw", "xw", "mw", "lw", "a16", "a17"):
+            fill(c(n), 0.0)
+        ts(c("cw", 4096, 4097), c("keq", 0, 1), NOB, A.mult)
+        ts(c("mw", 0, 1), c("keq", 0, 1), 16384.0, A.mult)
+        ts(c("bm"), c("cm"), col(6), A.is_equal)
+        for r in range(16):
+            ts(c("br", 128 * r, 128 * r + 128), c("bm"), c("keq", r, r + 1), A.mult)
+        cp(c("ni"), c("nlf"))
+        ts(c("na"), c("ni"), 127, A.bitwise_and)
+        cp(col(11), c("rth"))
+        ts(col(12), c("rth"), -2040.0, A.add)
+        for t in range(RO):
+            ts(c("tg"), c("na"), float(16 * t), A.is_equal, -30000.0, A.mult)
+            ts(c("thl", 256 * t, 256 * t + 256), c("tg"), col(12), A.add)
+        ts(c("rr"), c("jl"), 16.0, A.is_lt)
+        ts(c("pfr"), c("ci"), 1.0 / 512, A.mult)
+        ts(c("uo"), c("c16"), 16.0, A.mult, col(1), A.add)
+        ts(c("pll"), c("uo"), 256.0, A.add)
+        ts(c("pfl"), c("uo"), 1.0 / 512, A.mult)
+        ts(c("pv"), c("ci"), 1.0, A.add)
+        cp(c("tf"), c("rqs"))
+        conv_in("tf", "p5")
+        cp(c("qi"), c("tr"))
+        q_lists()
+
+    def bc16(out, src, buf):
+        cp(c(buf, 0, 256, 16), src)
+        scan(out, c("rr"), c(buf))
+
+    def q_update():
+        oh, q2 = c("tk", 0, 256), c("tk", 256, 512)
+        tt(q2, c("qd"), c("p5", 0, 256), A.add)
+        ts(q2, q2, 4096.0, A.min)
+        ts(c("sl", 0, 16), c("p5", 256, 272), 0.0, A.is_gt)
+        tt(c("sl", 0, 16), c("sl", 0, 16), c("wi"), A.mult)
+        tt(c("sl", 0, 16), c("sl", 0, 16), c("f16"), A.mult)
+        ts(c("sl", 16, 32), c("ui"), 16.0, A.mult, 16.0 - 4096.0, A.add)
+        tt(c("sl", 16, 32), c("sl", 16, 32), c("p5", 256, 272), A.subtract)
+        rep = c("p6", 256, 512)
+        bc16(rep, c("sl", 0, 16), "a16")
+        tt(oh, c("jl"), rep, A.is_equal)
+        bc16(rep, c("sl", 16, 32), "a17")
+        tt(c("p7", 0, 256), oh, rep, A.mult)
+        tt(c("qi"), q2, c("p7", 0, 256), A.add)
+
+    def x_lists():
+        ts(c("lvb"), c("lv"), 4608.0, A.mult)
+        tt(c("xl"), c("lvb"), c("p6", 256, 512), A.subtract)
+        dma("y", lane("xw", 0, 4096), c("xl"), "dxl")
+        cp(c("le"), c("p6", 256 + 15, 512, 16))
+        dma("y", lane("lw", 0, 256), c("le"), "dle")
+
+    def x_gather(q, k):
+        gat(q, c("xg", 1024 * k, 1024 * k + 1024), c("xw"), c("qdu", 64 * k, 64 * k + 64))
+
+    def x_ext(k):
+        ext(c("p5", 64 * k, 64 * k + 64), "za", "xg", 64 * k, 64)
+
+    def len_gather():
+        gat("s", c("lg"), c("lw"), c("uu"))
+
+    def len_ext():
+        ext(c("p5", 256, 272), "za", "lg", 0, 16)
+
+    for t in range(RO):
+        cp(c("ou"), c("oi"))
+        for k in range(4):
+            gat("s", c("wg", 1024 * k, 1024 * k + 1024), c("ww"), c("ou", 64 * k, 64 * k + 64))
+        ts(c("a2", 1, 256), c("ou", 0, 255), 2.0, A.mult, -1.0, A.add)
+        cp(c("a2", 0, 256, 16), c("hv"))
+        tt(c("t1"), c("a2"), c("p6", 0, 256), A.mult)
+        ts(c("t2"), c("t1"), 4, A.arith_shift_right)
+        tt(c("p7", 0, 256), c("t2"), c("p6", 0, 256), A.add)
+        ts(c("p37"), c("ou"), 37.0, A.mult, 77.0 * t - 37.0, A.add)
+        tt(c("hi", 0, 256), c("p37"), c("p7", 0, 256), A.add)
+        tt(pr("hi", 0, 8), pr("p37", 0), pr("p7", 1), A.add)
+        tt(pr("hi", 1, 8), pr("p37", 1), pr("p7", 0), A.add)
+        ts(c("hj"), c("hi"), 4095, A.bitwise_and)
+        cp(c("hu"), c("hj"))
+        for par in range(2):
+            ts(c("em", 128 * par, 128 * par + 128), pr("oi", par), 0.0, A.is_equal, 16384.0, A.mult)
+        o = c("p3", 0, 128)
+        mms([(o, c("idb"), c("em", 128 * par, 128 * par + 128), par == 0, par == 1) for par in range(2)], o)
+        if t:
+            x_lists()
+        for s in range(2):
+            for k in range(4):
+                w, h = c("wg", 1024 * k, 1024 * k + 1024), c("hu", 256 * s + 64 * k, 256 * s + 64 * k + 64)
+                m = c("mn", 4096 * s + 1024 * k, 4096 * s + 1024 * k + 1024)
+                run("v", [c("xs"), h, w], [m], lambda v: v.tensor_tensor(m[0], T.xs[:, 0:4096].indirect(h[0]), w[0], A.min))
+        if t:
+            for k in range(4):
+                x_gather("s", k)
+            len_gather()
+        for k in range(4):
+            ext(c("p0", 64 * k, 64 * k + 64), "zs", "mn", 64 * k, 64)
+        act(c("m1s"), c("p0", 0, 256))
+        for k in range(4):
+            if t:
+                x_ext(k)
+            ext(c("p1", 64 * k, 64 * k + 64), "zs", "mn", 256 + 64 * k, 64)
+        if t:
+            len_ext()
+        if t == 0:
+            more_constants()
+        tt(c("p7", 256, 512), c("p1", 0, 256), c("m1s"), A.subtract)
+        cp(c("dob"), pr("p7", 1, 8))
+        tt(c("ds"), pr("p7", 0, 8), c("dob"), A.add)
+        for par in range(2):
+            tt(pr("sw", par), c("ds"), c("p3", 0, 128), A.is_gt)
+        dma("y", lane("cw", 2, 4096), c("sw"), "dsw")
+        tt(c("p7", 0, 256), c("p7", 256, 512), c("sw"), A.mult)
+        tt(c("p7", 256, 512), c("p7", 0, 256), c("m1s"), A.add)
+        cp(c("chi"), c("p7", 256, 512))
+        dma("y", lane("cw", 0, 4096), c("chi"), "dhi")
+        tt(c("clo"), c("p7", 256, 512), c("chi"), A.subtract)
+        dma("s", lane("cw", 1, 4096), c("clo"), "dlo")
+        if t:
+            q_update()
+            q_lists()
+        for k in (0, 2, 1, 3):
+            gat("v" if k < 2 else "s", c("cg", 1024 * k, 1024 * k + 1024), c("cw"), c("qu", 64 * k, 64 * k + 64))
+            ext(c("p0", 256 + 64 * k, 256 + 64 * k + 64), "za", "cg", 64 * k, 64)
+        ext(c("p3", 256, 512), "zf", "cg", 0, 256)
+        cp(c("t8"), k3("p0", 8, 16, 16, 32))
+        tt(c("t8b"), k3("p0", 0, 8, 16, 32), c("t8"), A.max)
+        tt(c("t4"), k3("t8b", 0, 4), k3("t8b", 4, 8), A.max)
+        tt(c("t2x"), k3("t4", 0, 2), k3("t4", 2, 4), A.max)
+        mine = c("bs", 16 * t, 16 * t + 16)
+        tt(mine, k1("t2x", 0), k1("t2x", 1), A.max)
+        order("g", [mine], [])
+        others = [d for d in T.cores if d != core]
+        mask = 0xFFFFFFFF
+        for d in others:
+            mask &= topo.mask(core, d)
+        eng = bin(mask).count("1")
+        ids = []
+        for d in others:
+            rid, pid, _ = topo.addr(d)
+            ids.append(DstId(rid=rid, pnc=pid))
+        here = 64 * t + 16 * rank
+        g.remote_dma_fused([RemoteDMATransfer(dst_ids=ids, dma_engine_mask=mask, remote_sem=T.sem["arr%d" % t], srcs=[mine[0]],
+                                              dsts=[T.land[:, here:here + 16] for d in others])], local_sem=T.sem.snt)
+        cnt["snt"] += eng
+        cnt["arr%d" % t] = eng * (n_ranks - 1)
+        note("g", [], [c("land", 64 * t, 64 * t + 64)], "arr%d" % t, cnt["arr%d" % t])
+        act(c("cs"), c("p0", 256, 512), F.Identity, bias=col(11), scale=1.0)
+        fill(c("qw"), 0.0)
+        tt(c("p7", 0, 128), pr("oi", 1), pr("oi", 0), A.subtract)
+        tt(c("p7", 128, 256), c("p7", 0, 128), pr("sw", 0), A.mult)
+        tt(pr("o2", 0), c("p7", 128, 256), pr("oi", 0), A.add)
+        tt(pr("o2", 1), pr("oi", 1), c("p7", 128, 256), A.subtract)
+        cp(c("ou2"), c("o2"))
+        cp(c("ccs"), c("p7", 256, 512))
+        tt(c("p7", 0, 128), pr("p7", 1, 8), pr("ccs", 0), A.subtract)
+        tt(c("p7", 128, 256), c("p7", 0, 128), pr("sw", 0), A.mult)
+        tt(c("e1l"), c("ccs"), c("thl", 256 * t, 256 * t + 256), A.add)
+        tt(pr("c2l", 0), c("p7", 128, 256), pr("e1l", 0), A.add)
+        tt(pr("c2l", 1), pr("e1l", 1), c("p7", 128, 256), A.subtract)
+        ts(c("g32"), c("o2"), 32.0, A.mult)
+        tt(c("p7", 0, 256), c("p3", 256, 512), c("dq"), A.mult)
+        tt(c("qd"), c("p7", 0, 256), c("qi"), A.add)
+        cp(c("qdu"), c("qd"))
+        ts(c("hq"), c("qd"), 4096 + 127, A.bitwise_and)
+        ts(c("p7", 0, 256), c("hq"), float(16 * t), A.is_equal, -30000.0, A.mult)
+        tt(c("cx"), c("p7", 0, 256), c("cs"), A.add)
+        lands = [c("land", 64 * t + 16 * r, 64 * t + 16 * r + 16) for r in range(n_ranks)]
+        lower, higher = lands[:rank], lands[rank + 1:]
+        seq = lower + higher
+        tt(c("mm"), mine, seq[0], A.max)
+        for x in seq[1:]:
+            tt(c("mm"), c("mm"), x, A.max)
+        ts(c("m16"), c("mm"), -2040.0, A.add)
+        for r in range(16):
+            o = c("p4", r, 256, 16)
+            mms([(o, c("br", 128 * r, 128 * r + 128), c("m16"), True, True)], o)
+        ts(c("mt"), c("p4", 0, 256), c("keq", 1, 2), A.mult)
+        tt(c("mw", 1, 257), c("p4", 0, 256), c("mt"), A.subtract)
+        for k in range(3):
+            gat("s", c("mg", 1024 * k, 1024 * k + 1024), c("mw"), c("ou2", 64 * k, 64 * k + 64))
+        tt(c("s1"), c("mm"), c("ws"), A.add)
+        ts(c("ui"), c("s1"), 255, A.bitwise_and)
+        bc16(c("p6", 256, 512), c("mm"), "a16")
+        tt(c("p7", 256, 512), c("p6", 256, 512), c("cx"), A.is_gt)
+        tt(c("jv"), c("p7", 256, 512), c("jl"), A.mult)
+        tt(c("t8"), k3("jv", 0, 8), k3("jv", 8, 16), A.max)
+        tt(c("t4"), k3("t8", 0, 4), k3("t8", 4, 8), A.max)
+        tt(c("t2x"), k3("t4", 0, 2), k3("t4", 2, 4), A.max)
+        tt(c("f16"), k1("t2x", 0), k1("t2x", 1), A.max)
+        ts(c("va"), c("f16"), 0.0, A.is_gt)
+        tt(c("h1"), mine, c("mm"), A.is_equal)
+        tt(c("va"), c("va"), c("h1"), A.mult)
+        if lower:
+            top = lower[0]
+            for x in lower[1:]:
+                tt(c("lm"), top, x, A.max)
+                top = c("lm")
+            tt(c("h2"), top, c("mm"), A.is_lt)
+            tt(c("va"), c("va"), c("h2"), A.mult)
+        ts(c("vb"), c("ui"), -1024.0, A.add)
+        tt(c("vb"), c("vb"), c("va"), A.mult)
+        ts(c("uh"), c("vb"), 1024.0, A.add)
+        ts(c("uc"), c("vb"), 1024.0, A.add)
+        for r in range(16):
+            o = c("p4", 256 + r, 512, 16)
+            mms([(o, c("br", 128 * r, 128 * r + 128), c("uh"), True, True)], o)
+        for k in range(3):
+            ext(c("p4", 64 * k, 64 * k + 64), "za", "mg", 64 * k, 64)
+        tt(c("kr"), c("p4", 256, 512), c("pfr"), A.add)
+        cp(c("uu"), c("ui"))
+        for pc in range(16):
+            o = c("tk", 256 * (pc % 4), 256 * (pc % 4) + 16 * pc + 16)
+            ts(o, c("kr", 0, 16 * pc + 16), c("uc", pc, pc + 1), A.subtract)
+            d = c("res", pc, pc + 1)
+            run("v", [o], [d], lambda v: v.tensor_reduce(d[0], o[0], AxisListType.X, A.min, apply_absolute_value=True))
+        tt(c("wi"), c("res"), c("pfl"), A.is_equal)
+        tt(c("wi"), c("wi"), c("va"), A.mult)
+        tt(c("uo"), c("uc"), c("pll"), A.subtract)
+        tt(c("uo"), c("uo"), c("wi"), A.mult)
+        tt(c("uo"), c("uo"), c("pll"), A.add)
+        cp(c("uou"), c("uo"))
+        run("v", [c("pv"), c("uou")], [c("qw")], lambda v: v.tensor_copy(T.qw[:, 0:512].indirect(T.uou[:, 0:16]), T.pv[:, 0:256]))
+        o = c("p5", 288, 304)
+        mms([(o, c("zf", 15 - r, 143 - r), c("qw", 16 * r, 16 * r + 16), r == 0, r == 15) for r in range(16)], o)
+        gat("v", c("mg", 3072, 4096), c("mw"), c("ou2", 192, 256))
+        ext(c("p4", 192, 256), "za", "mg", 192, 64)
+        sh = c("p6", 256, 512)
+        tt(c("lv"), c("p4", 0, 256), c("c2l"), A.is_gt)
+        tt(c("st"), c("p4", 0, 256), c("c2l"), A.is_le)
+        scan(sh, c("rr"), c("lv"))
+        tt(c("p7", 256, 512), c("g32"), sh, A.add)
+        tt(k3("yb", 0, 16), c("p7", 256, 512), c("st"), A.mult)
+        gone = c("p6", 256 + 15, 512, 16)
+        ts(c("ap", 0, 16), gone, 0.0, A.is_gt)
+        tt(c("ap", 16, 32), c("p5", 288, 304), c("ap", 0, 16), A.mult)
+        ts(c("ap", 32, 48), c("ap", 16, 32), 0.0, A.is_gt)
+        tt(c("ap", 32, 48), c("ap", 32, 48), gone, A.mult)
+        ts(c("ap", 16, 32), c("ap", 16, 32), 32.0, A.mult)
+        tt(k1("yb", 16), c("ap", 16, 32), c("ap", 32, 48), A.add)
+        for b in range(5):
+            d = 1 << b
+            y, m, to = k3("yb", d, 17), k3("p2", d, 17), k3("yb", 0, 17 - d)
+            ts(k3("tb", d, 17), y, b, A.arith_shift_right, 1, A.bitwise_and)
+            tt(m, k3("tb", d, 17), y, A.mult)
+            tt(y, y, m, A.subtract)
+            tt(to, to, m, A.add)
+        ts(c("oi"), k3("yb", 0, 16), 5, A.arith_shift_right)
+    x_lists()
+    for k in (0, 2, 1, 3):
+        x_gather("v" if k < 2 else "s", k)
+        x_ext(k)
+    len_gather()
+    len_ext()
+    ts(c("tf"), c("oi"), 0.0, A.is_equal, 257.0, A.mult)
+    ts(c("tg"), c("oi"), -1.0, A.add)
+    tt(c("tr"), c("tf"), c("tg"), A.add)
+    conv_out("of", "p1")
+    for q in range(16):
+        cp(c("kr", q, 256, 16), c("of", 16 * q, 16 * q + 16))
+    dma("y", T.yoc[:, :], c("kr"), "dyo")
+    q_update()
+    cp(c("tr"), c("qi"))
+    conv_out("tg", "p1")
+    dma("y", T.yq[:, :], c("tg"), "dyq")
+    for s in SEMAPHORES:
+        if cnt[s] > known["g"].get(s, 0):
+            g.wait_ge(T.sem[s], cnt[s])

@@ -49,7 +49,9 @@ SCRATCH["p2"] = ("psum", [128, 16, 32], "float32")
 SCRATCH["p7"] = ("psum", [128, 16, 32], "float32")
 SEMAPHORES = ["sv", "ss", "st", "sg", "snt", "arr0", "arr1", "arr2", "arr3", "dx", "dw", "doc", "dqs", "dth",
               "dhi", "dlo", "dsw", "dxl", "dle", "dyo", "dyq"]
-QSEM = {"v": "sv", "s": "ss", "t": "st", "g": "sg"}
+QSEM = {"v": "sv", "s": "ss", "t": "st", "g": "sg", "n": ""}
+LANES = {"cw": ["cw_0", "cw_1", "cw_2"], "xw": ["xw_0"], "lw": ["lw_0"]}
+CY, WAKE, GATHER, EARLY, SPLIT = 0.00083, 0.15, 1.4, 0.0, True
 
 
 def rank_program(g, core, T, topo):
@@ -60,7 +62,7 @@ def rank_program(g, core, T, topo):
     queues = {"v": g.vector, "s": g.scalar, "t": g.tensor, "y": g.sync, "g": g}
     cnt = dict((s, 0) for s in SEMAPHORES)
     known = dict((q, {}) for q in queues)
-    log = dict((n, []) for n in SCRATCH)
+    log = dict((n, []) for n in list(SCRATCH) + ["wire"] + sum(LANES.values(), []))
     psum = set(n for n in SCRATCH if SCRATCH[n][0] == "psum")
 
     def c(name, a=0, b=None, step=1):
@@ -69,20 +71,23 @@ def rank_program(g, core, T, topo):
             w = shp[2]
             if b is None:
                 b = shp[1] * w
-            return (T[name][:, a // w:b // w, :], name, a, b)
+            return (T[name][:, a // w:b // w, :], name, a, b, b - a, lambda x, y: c(name, a + x, a + y))
         if b is None:
             b = shp[1]
-        return (T[name][:, a:b:step] if step > 1 else T[name][:, a:b], name, a, b)
+        return (T[name][:, a:b:step] if step > 1 else T[name][:, a:b], name, a, b, (b - a + step - 1) // step,
+                lambda x, y: c(name, a + x * step, min(b, a + y * step), step))
 
     def k3(name, lo, hi, r0=0, r1=None):
         shp = SCRATCH[name][1]
         if r1 is None:
             r1 = shp[1]
-        return (T[name][:, r0:r1, lo:hi], name, r0 * shp[2], r1 * shp[2])
+        w = hi - lo
+        return (T[name][:, r0:r1, lo:hi], name, r0 * shp[2], r1 * shp[2], (r1 - r0) * w,
+                lambda x, y: k3(name, lo, hi, r0 + x // w, r0 + y // w))
 
     def k1(name, j):
         shp = SCRATCH[name][1]
-        return (T[name][:, :, j], name, 0, shp[1] * shp[2])
+        return (T[name][:, :, j], name, 0, shp[1] * shp[2], shp[1], None)
 
     def pr(name, par, r0=0):
         return k3(name, 16 * par, 16 * par + 16, r0, r0 + 8)
@@ -90,7 +95,7 @@ def rank_program(g, core, T, topo):
     def order(q, rd, wr):
         need = {}
         for acc, isw in [(r, False) for r in rd] + [(w, True) for w in wr]:
-            _, name, lo, hi = acc
+            name, lo, hi = acc[1:4]
             for (l2, h2, w2, q2, sem, val) in log[name]:
                 if (name in psum and q2 != q) or (l2 < hi and lo < h2 and (isw or w2)):
                     if need.get(sem, 0) < val:
@@ -101,19 +106,20 @@ def rank_program(g, core, T, topo):
                 known[q][sem] = need[sem]
 
     def note(q, rd, wr, sem, val):
-        for (_, name, lo, hi) in rd:
+        for (name, lo, hi) in [r[1:4] for r in rd]:
             log[name] = [e for e in log[name] if not (e[3] == q and e[4] == sem and not e[2] and lo <= e[0] and e[1] <= hi)]
             log[name].append((lo, hi, False, q, sem, val))
-        for (_, name, lo, hi) in wr:
+        for (name, lo, hi) in [w[1:4] for w in wr]:
             log[name] = [e for e in log[name] if not (lo <= e[0] and e[1] <= hi and (name not in psum or e[3] == q))]
             log[name].append((lo, hi, True, q, sem, val))
 
-    def run(q, rd, wr, call):
-        order(q, rd, wr)
-        sem = QSEM[q]
-        cnt[sem] += 1
-        call(queues[q]).then_inc(T.sem[sem], 1)
-        note(q, rd, wr, sem, cnt[sem])
+    ops = []
+
+    def add(q, rd, wr, call, hold, sem=None, inc=1, lag=0.0):
+        ops.append((q, rd, wr, call, hold, sem or QSEM[q], inc, lag))
+
+    def run(q, rd, wr, call, n=64):
+        add(q, rd, wr, lambda e, s: call(e).then_inc(s, 1), CY * max(64, n))
 
     def cols(*xs):
         return [x for x in xs if isinstance(x, tuple)]
@@ -121,45 +127,100 @@ def rank_program(g, core, T, topo):
     def raw(x):
         return x[0] if isinstance(x, tuple) else x
 
+    def size(x):
+        return 2 if SCRATCH[x[1]][2] in ("bfloat16", "uint16", "float16") else 4
+
+    def parts(out, n, *xs):
+        if n < 128 or out[4] % 32 or not SPLIT or any(x[5] is None for x in (out,) + xs):
+            return [(out,) + xs]
+        h = out[4] // 2
+        return [tuple(x[5](a, a + h) for x in (out,) + xs) for a in (0, h)]
+
     def tt(out, a, b, op):
-        run("v", [a, b], [out], lambda v: v.tensor_tensor(out[0], a[0], b[0], op))
+        n = out[4] * (1 if a[1] in psum or b[1] in psum else 2)
+        for o, x, y in parts(out, n, a, b):
+            run("v", [x, y], [o], lambda v, o=o, x=x, y=y: v.tensor_tensor(o[0], x[0], y[0], op), n * o[4] // out[4])
 
     def ts(out, a, s1, op0, s2=None, op1=None):
-        if op1 is None:
-            run("v", [a] + cols(s1), [out], lambda v: v.tensor_scalar(out[0], a[0], raw(s1), None, op0))
-        else:
-            run("v", [a] + cols(s1, s2), [out], lambda v: v.tensor_scalar(out[0], a[0], raw(s1), raw(s2), op0, op1))
+        n = out[4] if size(out) + size(a) > 4 else out[4] // 2
+        for o, x in parts(out, n, a):
+            if op1 is None:
+                run("v", [x] + cols(s1), [o], lambda v, o=o, x=x: v.tensor_scalar(o[0], x[0], raw(s1), None, op0), n * o[4] // out[4])
+            else:
+                run("v", [x] + cols(s1, s2), [o], lambda v, o=o, x=x: v.tensor_scalar(o[0], x[0], raw(s1), raw(s2), op0, op1), n * o[4] // out[4])
 
     def cp(out, a):
-        run("v", [a], [out], lambda v: v.tensor_copy(out[0], a[0]))
+        n = out[4] if size(out) + size(a) > 4 else out[4] // 2
+        for o, x in parts(out, n, a):
+            run("v", [x], [o], lambda v, o=o, x=x: v.tensor_copy(o[0], x[0]), n * o[4] // out[4])
 
     def fill(out, x):
-        run("v", [], [out], lambda v: v.memset(out[0], x))
+        run("v", [], [out], lambda v: v.memset(out[0], x), out[4] // 2)
 
     def scan(out, d0, d1):
-        run("v", [d0, d1], [out], lambda v: v.tensor_tensor_scan(out[0], d0[0], d1[0], 0.0, A.mult, A.add))
+        for o, x, y in parts(out, out[4], d0, d1):
+            run("v", [x, y], [o], lambda v, o=o, x=x, y=y: v.tensor_tensor_scan(o[0], x[0], y[0], 0.0, A.mult, A.add), o[4])
 
     def act(out, a, func=F.Copy, **kw):
         k2 = dict((k, raw(kw[k])) for k in kw)
-        run("s", [a] + cols(*kw.values()), [out], lambda s: s.activation(out[0], a[0], func, **k2))
+        run("s", [a] + cols(*kw.values()), [out], lambda s: s.activation(out[0], a[0], func, **k2), 60 + out[4])
 
     def gat(q, out, win, off):
+        rd = [win, off] + [(None, x, 0, 9999) for x in LANES.get(win[1], [])]
         if q == "v":
-            run("v", [win, off], [out], lambda v: v.tensor_copy(out[0], win[0].indirect(off[0])))
+            run("v", rd, [out], lambda v: v.tensor_copy(out[0], win[0].indirect(off[0])), 60 + GATHER * out[4])
         else:
-            run("s", [win, off], [out], lambda s: s.activation(out[0], win[0].indirect(off[0]), F.Copy))
+            run("s", rd, [out], lambda s: s.activation(out[0], win[0].indirect(off[0]), F.Copy), 80 + GATHER * out[4])
 
     def mms(items, out):
         rd = []
         for it in items:
             rd += [it[1], it[2]]
-        order("t", rd, [out])
-        cnt["st"] += 1
-        for k, (o, l, r, a, b) in enumerate(items):
-            i = g.tensor.matmul(o[0], l[0], r[0], a, b)
-            if k == len(items) - 1:
-                i.then_inc(T.sem["st"], 1)
-        note("t", rd, [out], "st", cnt["st"])
+
+        def call(e, s):
+            for (o, l, r, a, b) in items:
+                i = e.matmul(o[0], l[0], r[0], a, b)
+            i.then_inc(s, 1)
+        add("t", rd, [out], call, CY * sum(max(64, r[4]) * (4 if size(r) == 4 else 1) for (_, _, r, _, _) in items))
+
+    def schedule():
+        n = len(ops)
+        pred, succ, seen = [], [[] for _ in range(n)], dict((b, []) for b in log)
+        for i, (q, rd, wr, call, hold, sem, inc, lag) in enumerate(ops):
+            p = set()
+            accs = [(r[1], r[2], r[3], False) for r in rd] + [(w[1], w[2], w[3], True) for w in wr]
+            for (name, lo, hi, w) in accs:
+                for (l2, h2, w2, q2, j) in seen[name]:
+                    if (name in psum and q2 != q) or (l2 < hi and lo < h2 and (w or w2)):
+                        p.add(j)
+            for (name, lo, hi, w) in accs:
+                seen[name] = [e for e in seen[name] if not (w and lo <= e[0] and e[1] <= hi and (name not in psum or e[3] == q))]
+                seen[name].append((lo, hi, w, q, i))
+            pred.append(p)
+            for j in p:
+                succ[j].append(i)
+        way = [0.0] * n
+        for i in range(n - 1, -1, -1):
+            way[i] = ops[i][4] + ops[i][7] + max([0.0] + [way[j] + WAKE for j in succ[i]])
+        left = [len(p) for p in pred]
+        ready = [0.0] * n
+        cand = set(i for i in range(n) if left[i] == 0)
+        free, seq = {}, []
+        while cand:
+            first = min(max(free.get(ops[i][0], 0.0), ready[i]) for i in cand)
+            now = [i for i in cand if max(free.get(ops[i][0], 0.0), ready[i]) <= first + EARLY]
+            best = max(now, key=lambda i: (way[i], -i))
+            cand.discard(best)
+            q, hold, lag = ops[best][0], ops[best][4], ops[best][7]
+            start = max(free.get(q, 0.0), ready[best])
+            free[q] = start + hold
+            seq.append(best)
+            for j in succ[best]:
+                ready[j] = max(ready[j], start + hold + lag + WAKE)
+                left[j] -= 1
+                if left[j] == 0:
+                    cand.add(j)
+        return seq
 
     def ext(out, z, name, c0, n):
         mms([(out, c(z, 15 - i, 143 - i), c(name, 16 * c0 + i, 16 * (c0 + n), 16), i == 0, i == 15) for i in range(16)], out)
@@ -167,13 +228,12 @@ def rank_program(g, core, T, topo):
     def dma(q, out, in_, sem):
         rd = cols(in_)
         wr = cols(out)
-        order(q, rd, wr)
-        cnt[sem] += 16
-        queues[q].dma_start(raw(out), raw(in_)).then_inc(T.sem[sem], 16)
-        note(q, rd, wr, sem, cnt[sem])
+        if wr and wr[0][1] in log and wr[0][1] not in SCRATCH:
+            rd = rd + [(None, wr[0][1][:-2], wr[0][2], wr[0][3])]
+        add(q, rd, wr, lambda e, s: e.dma_start(raw(out), raw(in_)).then_inc(s, 16), 0.1, sem, 16, 2.0)
 
     def lane(name, f, w):
-        return (T[name][f::16, 0:w], name, 0, w)
+        return (T[name][f::16, 0:w], "%s_%d" % (name, f), 0, w, 0, None)
 
     dma("y", c("roc"), T.oc[:, :], "doc")
     dma("y", c("rqs"), T.qs[:, :], "dqs")
@@ -230,14 +290,14 @@ def rank_program(g, core, T, topo):
     def conv_in(src, psname):
         for a in range(8):
             i, o = c(src, 32 * a, 32 * a + 32), flip(a)
-            run("v", [i], [o], lambda v: v.transpose(o[0], i[0]))
+            run("v", [i], [o], lambda v, i=i, o=o: v.transpose(o[0], i[0]))
         swap16(psname)
 
     def conv_out(dst, psname):
         swap16(psname)
         for a in range(8):
             o, i = c(dst, 32 * a, 32 * a + 32), flip(a)
-            run("v", [i], [o], lambda v: v.transpose(o[0], i[0]))
+            run("v", [i], [o], lambda v, i=i, o=o: v.transpose(o[0], i[0]))
 
     for q in range(16):
         cp(c("tf", 16 * q, 16 * q + 16), c("roc", q, 256, 16))
@@ -353,7 +413,8 @@ def rank_program(g, core, T, topo):
             for k in range(4):
                 w, h = c("wg", 1024 * k, 1024 * k + 1024), c("hu", 256 * s + 64 * k, 256 * s + 64 * k + 64)
                 m = c("mn", 4096 * s + 1024 * k, 4096 * s + 1024 * k + 1024)
-                run("v", [c("xs"), h, w], [m], lambda v: v.tensor_tensor(m[0], T.xs[:, 0:4096].indirect(h[0]), w[0], A.min))
+                run("v", [c("xs"), h, w], [m], lambda v, h=h, w=w, m=m: v.tensor_tensor(m[0], T.xs[:, 0:4096].indirect(h[0]), w[0], A.min),
+                    60 + GATHER * 1024)
         if t:
             for k in range(4):
                 x_gather("s", k)
@@ -394,7 +455,6 @@ def rank_program(g, core, T, topo):
         tt(c("t2x"), k3("t4", 0, 2), k3("t4", 2, 4), A.max)
         mine = c("bs", 16 * t, 16 * t + 16)
         tt(mine, k1("t2x", 0), k1("t2x", 1), A.max)
-        order("g", [mine], [])
         others = [d for d in T.cores if d != core]
         mask = 0xFFFFFFFF
         for d in others:
@@ -405,11 +465,11 @@ def rank_program(g, core, T, topo):
             rid, pid, _ = topo.addr(d)
             ids.append(DstId(rid=rid, pnc=pid))
         here = 64 * t + 16 * rank
-        g.remote_dma_fused([RemoteDMATransfer(dst_ids=ids, dma_engine_mask=mask, remote_sem=T.sem["arr%d" % t], srcs=[mine[0]],
-                                              dsts=[T.land[:, here:here + 16] for d in others])], local_sem=T.sem.snt)
-        cnt["snt"] += eng
-        cnt["arr%d" % t] = eng * (n_ranks - 1)
-        note("g", [], [c("land", 64 * t, 64 * t + 64)], "arr%d" % t, cnt["arr%d" % t])
+        send = RemoteDMATransfer(dst_ids=ids, dma_engine_mask=mask, remote_sem=T.sem["arr%d" % t], srcs=[mine[0]],
+                                 dsts=[T.land[:, here:here + 16] for d in others])
+        wire = (None, "wire", t, t + 1)
+        add("g", [mine], [wire], lambda e, s, send=send: e.remote_dma_fused([send], local_sem=s), 0.5, "snt", eng, 0.0)
+        add("n", [], [c("land", 64 * t, 64 * t + 64), wire], None, 0.0, "arr%d" % t, eng * (n_ranks - 1), 4.0)
         act(c("cs"), c("p0", 256, 512), F.Identity, bias=col(11), scale=1.0)
         fill(c("qw"), 0.0)
         tt(c("p7", 0, 128), pr("oi", 1), pr("oi", 0), A.subtract)
@@ -478,14 +538,14 @@ def rank_program(g, core, T, topo):
             o = c("tk", 256 * (pc % 4), 256 * (pc % 4) + 16 * pc + 16)
             ts(o, c("kr", 0, 16 * pc + 16), c("uc", pc, pc + 1), A.subtract)
             d = c("res", pc, pc + 1)
-            run("v", [o], [d], lambda v: v.tensor_reduce(d[0], o[0], AxisListType.X, A.min, apply_absolute_value=True))
+            run("v", [o], [d], lambda v, d=d, o=o: v.tensor_reduce(d[0], o[0], AxisListType.X, A.min, apply_absolute_value=True), 16 * pc + 16)
         tt(c("wi"), c("res"), c("pfl"), A.is_equal)
         tt(c("wi"), c("wi"), c("va"), A.mult)
         tt(c("uo"), c("uc"), c("pll"), A.subtract)
         tt(c("uo"), c("uo"), c("wi"), A.mult)
         tt(c("uo"), c("uo"), c("pll"), A.add)
         cp(c("uou"), c("uo"))
-        run("v", [c("pv"), c("uou")], [c("qw")], lambda v: v.tensor_copy(T.qw[:, 0:512].indirect(T.uou[:, 0:16]), T.pv[:, 0:256]))
+        run("v", [c("pv"), c("uou")], [c("qw")], lambda v: v.tensor_copy(T.qw[:, 0:512].indirect(T.uou[:, 0:16]), T.pv[:, 0:256]), 900)
         o = c("p5", 288, 304)
         mms([(o, c("zf", 15 - r, 143 - r), c("qw", 16 * r, 16 * r + 16), r == 0, r == 15) for r in range(16)], o)
         gat("v", c("mg", 3072, 4096), c("mw"), c("ou2", 192, 256))
@@ -528,6 +588,16 @@ def rank_program(g, core, T, topo):
     cp(c("tr"), c("qi"))
     conv_out("tg", "p1")
     dma("y", T.yq[:, :], c("tg"), "dyq")
+    for i in schedule():
+        q, rd, wr, call, hold, sem, inc, lag = ops[i]
+        if call is None:
+            cnt[sem] += inc
+            note(q, [], wr[:1], sem, cnt[sem])
+            continue
+        order(q, rd, wr)
+        cnt[sem] += inc
+        call(queues[q], T.sem[sem])
+        note(q, rd, wr, sem, cnt[sem])
     for s in SEMAPHORES:
         if cnt[s] > known["g"].get(s, 0):
             g.wait_ge(T.sem[s], cnt[s])

@@ -16,27 +16,27 @@ for _n, _w, _d in [
     ("zs", 144, "bfloat16"), ("za", 144, "bfloat16"), ("zf", 144, "bfloat16"), ("zw", 144, "bfloat16"),
     ("br", 2048, "float16"), ("bm", 128, "float32"), ("e0", 160, "float32"), ("e1", 160, "float32"),
     ("idb", 128, "bfloat16"),
-    ("ip", 1, "int32"), ("ki", 1, "int32"), ("gi", 1, "int32"), ("cf", 16, "float32"), ("keq", 16, "float32"),
-    ("ci", 256, "float32"), ("c16", 16, "float32"), ("cm", 128, "float32"), ("nlf", 256, "float32"), ("ni", 256, "int32"),
+    ("ip", 1, "int32"), ("ki", 1, "int32"), ("cf", 16, "float32"), ("keq", 16, "float32"),
+    ("ci", 256, "float32"), ("c16", 16, "float32"), ("ni", 256, "int32"), ("zn", 144, "bfloat16"), ("idn", 128, "bfloat16"), ("bo", 128, "bfloat16"),
+    ("lt", 256, "float32"), ("um", 256, "float32"), ("ub", 256, "bfloat16"), ("eqb", 2176, "bfloat16"), ("lz", 256, "bfloat16"), ("xo", 2048, "bfloat16"),
     ("na", 256, "int32"), ("thl", 1024, "float32"), ("jl", 256, "float32"), ("rr", 256, "float32"),
-    ("pfr", 256, "float32"), ("pfl", 16, "float32"), ("pll", 16, "float32"), ("pv", 256, "bfloat16"), ("ws", 16, "float32"),
+    ("pll", 16, "float32"), ("pv", 256, "bfloat16"), ("ws", 16, "float32"),
     ("hv", 16, "float32"), ("tf", 256, "float32"), ("tg", 256, "float32"), ("rt", 256, "float32"), ("of", 256, "float32"),
     ("ou", 256, "uint16"), ("ou2", 256, "uint16"),
     ("qi", 256, "int32"), ("qd", 256, "int32"), ("qu", 256, "uint16"), ("qdu", 256, "uint16"), ("dq", 256, "float32"), ("qa", 256, "int32"),
     ("a2", 256, "float32"), ("t1", 256, "int32"), ("t2", 256, "int32"), ("hj", 512, "int32"),
     ("hu", 512, "uint16"), ("em", 256, "bfloat16"),
     ("chi", 256, "bfloat16"), ("clo", 256, "bfloat16"), ("cs", 256, "float32"), ("cx", 256, "float32"),
-    ("g32", 256, "float32"), ("hq", 256, "int32"),
-    ("mm", 16, "float32"), ("m16", 16, "float16"), ("mt", 256, "bfloat16"), ("lm", 16, "float32"), ("h1", 16, "float32"), ("h2", 16, "float32"),
+    ("g32", 256, "float32"), ("fe", 256, "float32"), ("le32", 16, "float32"), ("hq", 256, "int32"),
+    ("mm", 16, "float32"), ("m16", 16, "float16"), ("mt", 256, "bfloat16"),
     ("s1", 16, "int32"), ("ui", 16, "int32"), ("a16", 256, "float32"), ("a17", 256, "float32"), ("f16", 16, "float32"),
-    ("va", 16, "float32"), ("vb", 16, "float32"), ("uc", 16, "float32"), ("uh", 16, "float16"), ("kr", 256, "float32"),
-    ("tk", 1024, "float32"), ("res", 16, "float32"), ("wi", 16, "float32"), ("uo", 16, "float32"), ("uou", 16, "uint16"), ("uu", 16, "uint16"),
+    ("va", 16, "float32"), ("vb", 16, "float32"), ("uc", 16, "float32"), ("uh", 16, "float16"), ("tk", 512, "float32"), ("wi", 16, "float32"), ("uo", 16, "float32"), ("uou", 16, "uint16"), ("uu", 16, "uint16"),
     ("lv", 256, "float32"), ("st", 256, "float32"), ("lvb", 256, "bfloat16"), ("xl", 256, "bfloat16"), ("le", 16, "bfloat16"),
     ("ap", 64, "float32"), ("sl", 64, "float32"), ("land", 256, "float32"), ("bs", 64, "float32"),
 ]:
     SCRATCH[_n] = ("sbuf", [128, _w], _d)
 for _n, _r, _w, _d in [
-    ("yb", 16, 17, "int32"), ("tb", 16, 17, "int32"), ("tr", 8, 32, "float32"), ("oi", 8, 32, "int32"), ("o2", 8, 32, "int32"),
+    ("yb", 16, 16, "int32"), ("tb", 16, 16, "int32"), ("tr", 8, 32, "float32"), ("oi", 8, 32, "int32"), ("o2", 8, 32, "int32"),
     ("hi", 16, 32, "int32"), ("p37", 8, 32, "float32"), ("m1s", 8, 32, "float32"), ("sw", 8, 32, "bfloat16"), ("ccs", 8, 32, "float32"),
     ("e1l", 8, 32, "float32"), ("c2l", 8, 32, "float32"), ("dob", 8, 16, "float32"), ("ds", 8, 16, "float32"),
     ("t8", 16, 8, "float32"), ("t8b", 16, 8, "float32"), ("t4", 16, 4, "float32"), ("t2x", 16, 2, "float32"), ("jv", 16, 16, "float32"),
@@ -52,6 +52,7 @@ SEMAPHORES = ["sv", "ss", "st", "sg", "snt", "arr0", "arr1", "arr2", "arr3", "dx
 QSEM = {"v": "sv", "s": "ss", "t": "st", "g": "sg", "n": ""}
 LANES = {"cw": ["cw_0", "cw_1", "cw_2"], "xw": ["xw_0"], "lw": ["lw_0"]}
 CY, WAKE, GATHER, EARLY, SPLIT = 0.00083, 0.15, 1.4, 0.0, True
+VIA = [(1, 3)]
 
 
 def rank_program(g, core, T, topo):
@@ -71,11 +72,11 @@ def rank_program(g, core, T, topo):
             w = shp[2]
             if b is None:
                 b = shp[1] * w
-            return (T[name][:, a // w:b // w, :], name, a, b, b - a, lambda x, y: c(name, a + x, a + y))
+            return (T[name][:, a // w:b // w, :], name, a, b, b - a, lambda x, y: c(name, a + x, a + y), w)
         if b is None:
             b = shp[1]
         return (T[name][:, a:b:step] if step > 1 else T[name][:, a:b], name, a, b, (b - a + step - 1) // step,
-                lambda x, y: c(name, a + x * step, min(b, a + y * step), step))
+                lambda x, y: c(name, a + x * step, min(b, a + y * step), step), 1)
 
     def k3(name, lo, hi, r0=0, r1=None):
         shp = SCRATCH[name][1]
@@ -83,7 +84,7 @@ def rank_program(g, core, T, topo):
             r1 = shp[1]
         w = hi - lo
         return (T[name][:, r0:r1, lo:hi], name, r0 * shp[2], r1 * shp[2], (r1 - r0) * w,
-                lambda x, y: k3(name, lo, hi, r0 + x // w, r0 + y // w))
+                lambda x, y: k3(name, lo, hi, r0 + x // w, r0 + y // w), w)
 
     def k1(name, j):
         shp = SCRATCH[name][1]
@@ -131,9 +132,9 @@ def rank_program(g, core, T, topo):
         return 2 if SCRATCH[x[1]][2] in ("bfloat16", "uint16", "float16") else 4
 
     def parts(out, n, *xs):
-        if n < 128 or out[4] % 32 or not SPLIT or any(x[5] is None for x in (out,) + xs):
-            return [(out,) + xs]
         h = out[4] // 2
+        if n < 128 or out[4] % 2 or not SPLIT or any(x[5] is None or h % x[6] for x in (out,) + xs):
+            return [(out,) + xs]
         return [tuple(x[5](a, a + h) for x in (out,) + xs) for a in (0, h)]
 
     def tt(out, a, b, op):
@@ -255,16 +256,17 @@ def rank_program(g, core, T, topo):
     iota(c("ci"), [[1, 256]], 0, 0)
     iota(c("c16"), [[1, 16]], 0, 0)
     iota(c("jl"), [[0, 16], [-1, 16]], 16, 0)
-    iota(c("cm"), [[16, 8], [0, 16]], 0, 0)
+    iota(c("um", 0, 128), [[16, 8], [0, 16]], 0, 0)
+    iota(c("lt"), [[0, 16], [1, 16]], 0, 0)
     ts(c("ki"), c("ip"), 15, A.bitwise_and)
-    tt(c("gi"), c("ip"), c("ki"), A.subtract)
+    tt(c("s1", 1, 2), c("ip"), c("ki"), A.subtract)
     cp(col(0), c("ip"))
     cp(col(1), c("ki"))
-    ts(col(2), c("gi"), 15.0, A.add)
+    ts(col(2), c("s1", 1, 2), 15.0, A.add)
     ts(col(3), c("ip"), 16.0, A.add)
     ts(col(4), c("ki"), 256.0, A.mult)
     ts(col(5), c("ki"), 32.0, A.mult, 1.0, A.add)
-    cp(col(6), c("gi"))
+    cp(col(6), c("s1", 1, 2))
     ts(col(10), c("ki"), 16.0, A.mult)
     ts(c("s1", 0, 1), c("ip"), 16, A.bitwise_and)
     ts(col(8), c("s1", 0, 1), 1.0 / 16, A.mult)
@@ -306,11 +308,12 @@ def rank_program(g, core, T, topo):
     ts(c("tg"), c("of"), 256.0, A.is_lt)
     ts(c("of"), c("of"), 1.0, A.add)
     tt(c("oi"), c("of"), c("tg"), A.mult)
-    ts(c("nlf"), c("ci"), col(4), A.add)
-    cp(c("p6", 0, 256), c("nlf"))
+    ts(c("p6", 0, 256), c("ci"), col(4), A.add)
     ts(c("hv"), c("c16"), 2.0, A.mult, col(5), A.add)
     ts(c("zs"), c("ci", 0, 144), col(2), A.is_equal)
+    ts(c("zn"), c("zs"), -1.0, A.mult)
     ts(c("idb"), c("ci", 0, 128), col(0), A.is_equal)
+    ts(c("idn"), c("idb"), -1.0, A.mult)
 
     def q_lists():
         cp(c("qu"), c("qi"))
@@ -328,10 +331,10 @@ def rank_program(g, core, T, topo):
             fill(c(n), 0.0)
         ts(c("cw", 4096, 4097), c("keq", 0, 1), NOB, A.mult)
         ts(c("mw", 0, 1), c("keq", 0, 1), 16384.0, A.mult)
-        ts(c("bm"), c("cm"), col(6), A.is_equal)
+        ts(c("bm"), c("um", 0, 128), col(6), A.is_equal)
         for r in range(16):
             ts(c("br", 128 * r, 128 * r + 128), c("bm"), c("keq", r, r + 1), A.mult)
-        cp(c("ni"), c("nlf"))
+        ts(c("ni"), c("ci"), col(4), A.add)
         ts(c("na"), c("ni"), 127, A.bitwise_and)
         cp(col(11), c("rth"))
         ts(col(12), c("rth"), -2040.0, A.add)
@@ -339,10 +342,10 @@ def rank_program(g, core, T, topo):
             ts(c("tg"), c("na"), float(16 * t), A.is_equal, -30000.0, A.mult)
             ts(c("thl", 256 * t, 256 * t + 256), c("tg"), col(12), A.add)
         ts(c("rr"), c("jl"), 16.0, A.is_lt)
-        ts(c("pfr"), c("ci"), 1.0 / 512, A.mult)
         ts(c("uo"), c("c16"), 16.0, A.mult, col(1), A.add)
         ts(c("pll"), c("uo"), 256.0, A.add)
-        ts(c("pfl"), c("uo"), 1.0 / 512, A.mult)
+        ts(c("lt"), c("lt"), col(1), A.is_le, 2048.0, A.mult)
+        cp(c("bo"), c("bm"))
         ts(c("pv"), c("ci"), 1.0, A.add)
         cp(c("tf"), c("rqs"))
         conv_in("tf", "p5")
@@ -373,7 +376,8 @@ def rank_program(g, core, T, topo):
         ts(c("lvb"), c("lv"), 4608.0, A.mult)
         tt(c("xl"), c("lvb"), c("p6", 256, 512), A.subtract)
         dma("y", lane("xw", 0, 4096), c("xl"), "dxl")
-        cp(c("le"), c("p6", 256 + 15, 512, 16))
+        cp(c("le32"), c("p6", 256 + 15, 512, 16))
+        cp(c("le"), c("le32"))
         dma("y", lane("lw", 0, 256), c("le"), "dle")
 
     def x_gather(q, k):
@@ -407,27 +411,34 @@ def rank_program(g, core, T, topo):
             ts(c("em", 128 * par, 128 * par + 128), pr("oi", par), 0.0, A.is_equal, 16384.0, A.mult)
         o = c("p3", 0, 128)
         mms([(o, c("idb"), c("em", 128 * par, 128 * par + 128), par == 0, par == 1) for par in range(2)], o)
-        if t:
-            x_lists()
         for s in range(2):
             for k in range(4):
                 w, h = c("wg", 1024 * k, 1024 * k + 1024), c("hu", 256 * s + 64 * k, 256 * s + 64 * k + 64)
                 m = c("mn", 4096 * s + 1024 * k, 4096 * s + 1024 * k + 1024)
+                if (s, k) in VIA:
+                    xo = 1024 * VIA.index((s, k))
+                    gat("s", c("xo", xo, xo + 1024), c("xs"), h)
+                    for j in range(2):
+                        o = c(("p2", "p4")[j], 0, 512)
+                        mms([(o, c("idb"), w[5](512 * j, 512 * j + 512), True, False),
+                             (o, c("idn"), c("xo", xo + 512 * j, xo + 512 * j + 512), False, True)], o)
+                        act(m[5](512 * j, 512 * j + 512), o, F.Relu)
+                    continue
                 run("v", [c("xs"), h, w], [m], lambda v, h=h, w=w, m=m: v.tensor_tensor(m[0], T.xs[:, 0:4096].indirect(h[0]), w[0], A.min),
                     60 + GATHER * 1024)
-        if t:
-            for k in range(4):
-                x_gather("s", k)
-            len_gather()
+        def score(s, k):
+            o = c("p%d" % s, 64 * k, 64 * k + 64)
+            if (s, k) in VIA:
+                items = [(o, c("zs", 15 - i, 143 - i), c("wg", 1024 * k + i, 1024 * k + 1024, 16), i == 0, False) for i in range(16)]
+                a = 4096 * s + 1024 * k
+                mms(items + [(o, c("zn", 15 - i, 143 - i), c("mn", a + i, a + 1024, 16), False, i == 15) for i in range(16)], o)
+            else:
+                ext(o, "zs", "mn", 256 * s + 64 * k, 64)
         for k in range(4):
-            ext(c("p0", 64 * k, 64 * k + 64), "zs", "mn", 64 * k, 64)
+            score(0, k)
         act(c("m1s"), c("p0", 0, 256))
         for k in range(4):
-            if t:
-                x_ext(k)
-            ext(c("p1", 64 * k, 64 * k + 64), "zs", "mn", 256 + 64 * k, 64)
-        if t:
-            len_ext()
+            score(1, k)
         if t == 0:
             more_constants()
         tt(c("p7", 256, 512), c("p1", 0, 256), c("m1s"), A.subtract)
@@ -483,7 +494,7 @@ def rank_program(g, core, T, topo):
         tt(c("e1l"), c("ccs"), c("thl", 256 * t, 256 * t + 256), A.add)
         tt(pr("c2l", 0), c("p7", 128, 256), pr("e1l", 0), A.add)
         tt(pr("c2l", 1), pr("e1l", 1), c("p7", 128, 256), A.subtract)
-        ts(c("g32"), c("o2"), 32.0, A.mult)
+        ts(c("g32"), c("o2"), 16.0, A.mult)
         tt(c("p7", 0, 256), c("p3", 256, 512), c("dq"), A.mult)
         tt(c("qd"), c("p7", 0, 256), c("qi"), A.add)
         cp(c("qdu"), c("qd"))
@@ -514,33 +525,41 @@ def rank_program(g, core, T, topo):
         tt(c("t2x"), k3("t4", 0, 2), k3("t4", 2, 4), A.max)
         tt(c("f16"), k1("t2x", 0), k1("t2x", 1), A.max)
         ts(c("va"), c("f16"), 0.0, A.is_gt)
-        tt(c("h1"), mine, c("mm"), A.is_equal)
-        tt(c("va"), c("va"), c("h1"), A.mult)
+        h1, h2, lm = c("sl", 32, 48), c("sl", 48, 64), c("ap", 48, 64)
+        tt(h1, mine, c("mm"), A.is_equal)
         if lower:
             top = lower[0]
             for x in lower[1:]:
-                tt(c("lm"), top, x, A.max)
-                top = c("lm")
-            tt(c("h2"), top, c("mm"), A.is_lt)
-            tt(c("va"), c("va"), c("h2"), A.mult)
+                tt(lm, top, x, A.max)
+                top = lm
+            tt(h2, top, c("mm"), A.is_lt)
+            tt(h1, h1, h2, A.mult)
+        tt(c("va"), c("va"), h1, A.mult)
         ts(c("vb"), c("ui"), -1024.0, A.add)
         tt(c("vb"), c("vb"), c("va"), A.mult)
         ts(c("uh"), c("vb"), 1024.0, A.add)
         ts(c("uc"), c("vb"), 1024.0, A.add)
         for r in range(16):
-            o = c("p4", 256 + r, 512, 16)
+            o = c("p3", r, 256, 16)
             mms([(o, c("br", 128 * r, 128 * r + 128), c("uh"), True, True)], o)
         for k in range(3):
             ext(c("p4", 64 * k, 64 * k + 64), "za", "mg", 64 * k, 64)
-        tt(c("kr"), c("p4", 256, 512), c("pfr"), A.add)
         cp(c("uu"), c("ui"))
-        for pc in range(16):
-            o = c("tk", 256 * (pc % 4), 256 * (pc % 4) + 16 * pc + 16)
-            ts(o, c("kr", 0, 16 * pc + 16), c("uc", pc, pc + 1), A.subtract)
-            d = c("res", pc, pc + 1)
-            run("v", [o], [d], lambda v, d=d, o=o: v.tensor_reduce(d[0], o[0], AxisListType.X, A.min, apply_absolute_value=True), 16 * pc + 16)
-        tt(c("wi"), c("res"), c("pfl"), A.is_equal)
-        tt(c("wi"), c("wi"), c("va"), A.mult)
+        cp(c("ub"), c("p3", 0, 256))
+        tt(c("um"), c("p3", 0, 256), c("lt"), A.add)
+        bc16(c("p6", 256, 512), c("uc"), "a16")
+        tt(c("eqb", 1920, 2176), c("um"), c("p6", 256, 512), A.is_equal)
+        at, los = [], [(c("p1", 0, 256), c("bo"), c("eqb", 1920, 2176))]
+        for pc in range(15):
+            a = sum(240 - 16 * z for z in range(pc))
+            o = c("eqb", a, a + 240 - 16 * pc)
+            ts(o, c("ub", 16 * pc + 16, 256), c("uc", pc, pc + 1), A.is_equal)
+            los.append((c("p1", 16 * pc + 16, 256), c("bo"), o))
+        for a, b in ((0, 6), (6, 11), (11, 16)):
+            mms([(los[z] + (z == 0, z == 15)) for z in range(a, b)], c("p1", 0, 256))
+        ts(c("lz"), c("p1", 0, 256), 0.0, A.is_equal)
+        ext(c("p5", 272, 288), "zf", "lz", 0, 16)
+        tt(c("wi"), c("va"), c("p5", 272, 288), A.mult)
         tt(c("uo"), c("uc"), c("pll"), A.subtract)
         tt(c("uo"), c("uo"), c("wi"), A.mult)
         tt(c("uo"), c("uo"), c("pll"), A.add)
@@ -555,35 +574,34 @@ def rank_program(g, core, T, topo):
         tt(c("st"), c("p4", 0, 256), c("c2l"), A.is_le)
         scan(sh, c("rr"), c("lv"))
         tt(c("p7", 256, 512), c("g32"), sh, A.add)
-        tt(k3("yb", 0, 16), c("p7", 256, 512), c("st"), A.mult)
-        gone = c("p6", 256 + 15, 512, 16)
-        ts(c("ap", 0, 16), gone, 0.0, A.is_gt)
-        tt(c("ap", 16, 32), c("p5", 288, 304), c("ap", 0, 16), A.mult)
-        ts(c("ap", 32, 48), c("ap", 16, 32), 0.0, A.is_gt)
-        tt(c("ap", 32, 48), c("ap", 32, 48), gone, A.mult)
-        ts(c("ap", 16, 32), c("ap", 16, 32), 32.0, A.mult)
-        tt(k1("yb", 16), c("ap", 16, 32), c("ap", 32, 48), A.add)
-        for b in range(5):
+        tt(c("yb"), c("p7", 256, 512), c("st"), A.mult)
+        x_lists()
+        bc16(sh, c("le32"), "a17")
+        tt(c("fe"), c("jl"), sh, A.is_equal)
+        for b in range(4):
             d = 1 << b
-            y, m, to = k3("yb", d, 17), k3("p2", d, 17), k3("yb", 0, 17 - d)
-            ts(k3("tb", d, 17), y, b, A.arith_shift_right, 1, A.bitwise_and)
-            tt(m, k3("tb", d, 17), y, A.mult)
+            y, m, to = k3("yb", d, 16), k3("p2", d, 16), k3("yb", 0, 16 - d)
+            ts(k3("tb", d, 16), y, b, A.arith_shift_right, 1, A.bitwise_and)
+            tt(m, k3("tb", d, 16), y, A.mult)
             tt(y, y, m, A.subtract)
             tt(to, to, m, A.add)
-        ts(c("oi"), k3("yb", 0, 16), 5, A.arith_shift_right)
-    x_lists()
-    for k in (0, 2, 1, 3):
-        x_gather("v" if k < 2 else "s", k)
-        x_ext(k)
-    len_gather()
-    len_ext()
+        ts(c("yb"), c("yb"), 4, A.arith_shift_right)
+        cp(c("ap", 0, 16), c("p5", 288, 304))
+        bc16(sh, c("ap", 0, 16), "a16")
+        tt(c("p7", 0, 256), c("fe"), sh, A.mult)
+        tt(c("oi"), c("yb"), c("p7", 0, 256), A.add)
+        for k in range(4):
+            x_gather("v" if t == RO - 1 and k == 3 else "s", k)
+            x_ext(k)
+        len_gather()
+        len_ext()
     ts(c("tf"), c("oi"), 0.0, A.is_equal, 257.0, A.mult)
     ts(c("tg"), c("oi"), -1.0, A.add)
     tt(c("tr"), c("tf"), c("tg"), A.add)
     conv_out("of", "p1")
     for q in range(16):
-        cp(c("kr", q, 256, 16), c("of", 16 * q, 16 * q + 16))
-    dma("y", T.yoc[:, :], c("kr"), "dyo")
+        cp(c("um", q, 256, 16), c("of", 16 * q, 16 * q + 16))
+    dma("y", T.yoc[:, :], c("um"), "dyo")
     q_update()
     cp(c("tr"), c("qi"))
     conv_out("tg", "p1")

@@ -14,7 +14,7 @@ for _n, _w, _d in [
     ("qw", 512, "bfloat16"),
     ("roc", 256, "int32"), ("rqs", 256, "int32"), ("rth", 1, "int32"),
     ("zs", 144, "bfloat16"), ("za", 144, "bfloat16"), ("zf", 144, "bfloat16"), ("zw", 144, "bfloat16"),
-    ("br", 2048, "float16"), ("bm", 128, "float32"), ("e0", 160, "float32"), ("e1", 160, "float32"),
+    ("br", 2048, "float16"), ("e0", 160, "float32"), ("e1", 160, "float32"),
     ("idb", 128, "bfloat16"),
     ("ip", 1, "int32"), ("ki", 1, "int32"), ("cf", 16, "float32"), ("keq", 16, "float32"),
     ("ci", 256, "float32"), ("c16", 16, "float32"), ("ni", 256, "int32"), ("zn", 144, "bfloat16"), ("idn", 128, "bfloat16"), ("bo", 128, "bfloat16"),
@@ -23,7 +23,7 @@ for _n, _w, _d in [
     ("pll", 16, "float32"), ("pv", 256, "bfloat16"), ("ws", 16, "float32"),
     ("hv", 16, "float32"), ("tf", 256, "float32"), ("tg", 256, "float32"), ("rt", 256, "float32"), ("of", 256, "float32"),
     ("ou", 256, "uint16"), ("ou2", 256, "uint16"),
-    ("qi", 256, "int32"), ("qd", 256, "int32"), ("qu", 256, "uint16"), ("qdu", 256, "uint16"), ("dq", 256, "float32"), ("qa", 256, "int32"),
+    ("qi", 256, "int32"), ("qd", 256, "int32"), ("qu", 256, "uint16"), ("qdu", 256, "uint16"), ("ko", 256, "float32"),
     ("a2", 256, "float32"), ("t1", 256, "int32"), ("t2", 256, "int32"), ("hj", 512, "int32"),
     ("hu", 512, "uint16"), ("em", 256, "bfloat16"),
     ("chi", 256, "bfloat16"), ("clo", 256, "bfloat16"), ("cs", 256, "float32"), ("cx", 256, "float32"),
@@ -36,7 +36,7 @@ for _n, _w, _d in [
 ]:
     SCRATCH[_n] = ("sbuf", [128, _w], _d)
 for _n, _r, _w, _d in [
-    ("yb", 16, 16, "int32"), ("tb", 16, 16, "int32"), ("tr", 8, 32, "float32"), ("oi", 8, 32, "int32"), ("o2", 8, 32, "int32"),
+    ("yb", 16, 16, "int32"), ("tb", 16, 16, "int32"), ("tr", 8, 32, "float32"), ("oi", 8, 32, "float32"), ("swd", 8, 32, "bfloat16"), ("o2", 8, 32, "int32"),
     ("hi", 16, 32, "int32"), ("p37", 8, 32, "float32"), ("m1s", 8, 32, "float32"), ("sw", 8, 32, "bfloat16"), ("ccs", 8, 32, "float32"),
     ("e1l", 8, 32, "float32"), ("c2l", 8, 32, "float32"), ("dob", 8, 16, "float32"), ("ds", 8, 16, "float32"),
     ("t8", 16, 8, "float32"), ("t8b", 16, 8, "float32"), ("t4", 16, 4, "float32"), ("t2x", 16, 2, "float32"), ("jv", 16, 16, "float32"),
@@ -52,7 +52,9 @@ SEMAPHORES = ["sv", "ss", "st", "sg", "snt", "arr0", "arr1", "arr2", "arr3", "dx
 QSEM = {"v": "sv", "s": "ss", "t": "st", "g": "sg", "n": ""}
 LANES = {"cw": ["cw_0", "cw_1", "cw_2"], "xw": ["xw_0"], "lw": ["lw_0"]}
 CY, WAKE, GATHER, EARLY, SPLIT = 0.00083, 0.15, 1.4, 0.0, True
-VIA = [(1, 3)]
+PIECES = [(0, 0, 64, 0), (0, 64, 64, 0), (0, 128, 64, 0), (0, 192, 64, 0), (1, 192, 64, 1), (1, 0, 64, 0), (1, 64, 64, 0), (1, 128, 64, 0)]
+BOOST = [0.0, 3.0, 6.0, 0.0, 9.0]
+MPIECES = [("s", 0, 64), ("s", 64, 64), ("s", 128, 64), ("v", 192, 64)]
 
 
 def rank_program(g, core, T, topo):
@@ -76,7 +78,7 @@ def rank_program(g, core, T, topo):
         if b is None:
             b = shp[1]
         return (T[name][:, a:b:step] if step > 1 else T[name][:, a:b], name, a, b, (b - a + step - 1) // step,
-                lambda x, y: c(name, a + x * step, min(b, a + y * step), step), 1)
+                lambda x, y: c(name, a + x * step, min(b, a + y * step), step), 1, step)
 
     def k3(name, lo, hi, r0=0, r1=None):
         shp = SCRATCH[name][1]
@@ -93,12 +95,25 @@ def rank_program(g, core, T, topo):
     def pr(name, par, r0=0):
         return k3(name, 16 * par, 16 * par + 16, r0, r0 + 8)
 
+    def region(x, isw):
+        return (x[1], x[2], x[3], x[7] if len(x) > 7 else 1, isw)
+
+    def meet(x, e, q):
+        name, lo, hi, st, w = x
+        if name in psum and e[4] != q:
+            return True
+        return e[0] < hi and lo < e[1] and (w or e[3]) and not (st > 1 and st == e[2] and (lo - e[0]) % st)
+
+    def covered(x, e, q):
+        name, lo, hi, st, w = x
+        return lo <= e[0] and e[1] <= hi and (st == 1 or (st == e[2] and lo == e[0])) and (w or not e[3]) and (e[4] == q or (w and name not in psum))
+
     def order(q, rd, wr):
         need = {}
-        for acc, isw in [(r, False) for r in rd] + [(w, True) for w in wr]:
-            name, lo, hi = acc[1:4]
-            for (l2, h2, w2, q2, sem, val) in log[name]:
-                if (name in psum and q2 != q) or (l2 < hi and lo < h2 and (isw or w2)):
+        for x in [region(r, False) for r in rd] + [region(w, True) for w in wr]:
+            for e in log[x[0]]:
+                if meet(x, e, q):
+                    sem, val = e[5:]
                     if need.get(sem, 0) < val:
                         need[sem] = val
         for sem in sorted(need):
@@ -107,17 +122,14 @@ def rank_program(g, core, T, topo):
                 known[q][sem] = need[sem]
 
     def note(q, rd, wr, sem, val):
-        for (name, lo, hi) in [r[1:4] for r in rd]:
-            log[name] = [e for e in log[name] if not (e[3] == q and e[4] == sem and not e[2] and lo <= e[0] and e[1] <= hi)]
-            log[name].append((lo, hi, False, q, sem, val))
-        for (name, lo, hi) in [w[1:4] for w in wr]:
-            log[name] = [e for e in log[name] if not (lo <= e[0] and e[1] <= hi and (name not in psum or e[3] == q))]
-            log[name].append((lo, hi, True, q, sem, val))
+        for x in [region(r, False) for r in rd] + [region(w, True) for w in wr]:
+            log[x[0]] = [e for e in log[x[0]] if not (covered(x, e, q) and (x[4] or e[5] == sem))]
+            log[x[0]].append(x[1:] + (q, sem, val))
 
-    ops = []
+    ops, boost = [], [0.0]
 
     def add(q, rd, wr, call, hold, sem=None, inc=1, lag=0.0):
-        ops.append((q, rd, wr, call, hold, sem or QSEM[q], inc, lag))
+        ops.append((q, rd, wr, call, hold, sem or QSEM[q], inc, lag, boost[0]))
 
     def run(q, rd, wr, call, n=64):
         add(q, rd, wr, lambda e, s: call(e).then_inc(s, 1), CY * max(64, n))
@@ -187,16 +199,14 @@ def rank_program(g, core, T, topo):
     def schedule():
         n = len(ops)
         pred, succ, seen = [], [[] for _ in range(n)], dict((b, []) for b in log)
-        for i, (q, rd, wr, call, hold, sem, inc, lag) in enumerate(ops):
+        for i, (q, rd, wr) in enumerate(op[:3] for op in ops):
             p = set()
-            accs = [(r[1], r[2], r[3], False) for r in rd] + [(w[1], w[2], w[3], True) for w in wr]
-            for (name, lo, hi, w) in accs:
-                for (l2, h2, w2, q2, j) in seen[name]:
-                    if (name in psum and q2 != q) or (l2 < hi and lo < h2 and (w or w2)):
-                        p.add(j)
-            for (name, lo, hi, w) in accs:
-                seen[name] = [e for e in seen[name] if not (w and lo <= e[0] and e[1] <= hi and (name not in psum or e[3] == q))]
-                seen[name].append((lo, hi, w, q, i))
+            accs = [region(r, False) for r in rd] + [region(w, True) for w in wr]
+            for x in accs:
+                p.update(e[5] for e in seen[x[0]] if meet(x, e, q))
+            for x in accs:
+                seen[x[0]] = [e for e in seen[x[0]] if not (x[4] and covered(x, e, q))]
+                seen[x[0]].append(x[1:] + (q, i))
             pred.append(p)
             for j in p:
                 succ[j].append(i)
@@ -210,7 +220,7 @@ def rank_program(g, core, T, topo):
         while cand:
             first = min(max(free.get(ops[i][0], 0.0), ready[i]) for i in cand)
             now = [i for i in cand if max(free.get(ops[i][0], 0.0), ready[i]) <= first + EARLY]
-            best = max(now, key=lambda i: (way[i], -i))
+            best = max(now, key=lambda i: (way[i] + ops[i][8], -i))
             cand.discard(best)
             q, hold, lag = ops[best][0], ops[best][4], ops[best][7]
             start = max(free.get(q, 0.0), ready[best])
@@ -247,7 +257,7 @@ def rank_program(g, core, T, topo):
         if SCRATCH[out[1]][2] == "int32":
             run("g", [], [out], lambda e: e.iota(out[0], pattern, base, cm))
         else:
-            run("g", [], [out], lambda e: e.iota(out[0], pattern, base, cm, allow_small_or_imprecise_dtypes=True))
+            run("g", [], [out], lambda e: e.iota(out[0], pattern, base, cm, allow_small_or_imprecise_dtypes=True), 160 + 2 * out[4])
 
     def col(j):
         return c("cf", j, j + 1)
@@ -258,6 +268,9 @@ def rank_program(g, core, T, topo):
     iota(c("jl"), [[0, 16], [-1, 16]], 16, 0)
     iota(c("um", 0, 128), [[16, 8], [0, 16]], 0, 0)
     iota(c("lt"), [[0, 16], [1, 16]], 0, 0)
+    iota(c("cw"), [[0, 4112]], 0, 0)
+    iota(c("pv"), [[1, 256]], 1, 0)
+    iota(c("xw"), [[0, 4112]], 0, 0)
     ts(c("ki"), c("ip"), 15, A.bitwise_and)
     tt(c("s1", 1, 2), c("ip"), c("ki"), A.subtract)
     cp(col(0), c("ip"))
@@ -317,8 +330,6 @@ def rank_program(g, core, T, topo):
 
     def q_lists():
         cp(c("qu"), c("qi"))
-        ts(c("qa"), c("qi"), 16, A.bitwise_and)
-        ts(c("dq"), c("qa"), -2.0, A.mult, 16.0, A.add)
 
     def more_constants():
         ts(c("za"), c("ci", 0, 144), col(2), A.is_equal, col(9), A.mult)
@@ -327,26 +338,26 @@ def rank_program(g, core, T, topo):
         o = c("p5", 0, 16)
         mms([(o, c("zw", 15 - i, 143 - i), c("ww", 1 + i, 257, 16), i == 0, i == 15) for i in range(16)], o)
         cp(c("ws"), o)
-        for n in ("cw", "xw", "mw", "lw", "a16", "a17"):
+        for n in ("mw", "lw", "a16", "a17"):
             fill(c(n), 0.0)
         ts(c("cw", 4096, 4097), c("keq", 0, 1), NOB, A.mult)
         ts(c("mw", 0, 1), c("keq", 0, 1), 16384.0, A.mult)
-        ts(c("bm"), c("um", 0, 128), col(6), A.is_equal)
+        ts(c("bo"), c("um", 0, 128), col(6), A.is_equal)
         for r in range(16):
-            ts(c("br", 128 * r, 128 * r + 128), c("bm"), c("keq", r, r + 1), A.mult)
+            ts(c("br", 128 * r, 128 * r + 128), c("bo"), c("keq", r, r + 1), A.mult)
         ts(c("ni"), c("ci"), col(4), A.add)
         ts(c("na"), c("ni"), 127, A.bitwise_and)
         cp(col(11), c("rth"))
         ts(col(12), c("rth"), -2040.0, A.add)
         for t in range(RO):
-            ts(c("tg"), c("na"), float(16 * t), A.is_equal, -30000.0, A.mult)
-            ts(c("thl", 256 * t, 256 * t + 256), c("tg"), col(12), A.add)
+            x = c("thl", 256 * t, 256 * t + 256)
+            ts(x, c("na"), float(16 * t), A.is_equal, -30000.0, A.mult)
+            act(x, x, F.Identity, bias=col(12), scale=1.0)
         ts(c("rr"), c("jl"), 16.0, A.is_lt)
         ts(c("uo"), c("c16"), 16.0, A.mult, col(1), A.add)
         ts(c("pll"), c("uo"), 256.0, A.add)
         ts(c("lt"), c("lt"), col(1), A.is_le, 2048.0, A.mult)
-        cp(c("bo"), c("bm"))
-        ts(c("pv"), c("ci"), 1.0, A.add)
+        ts(c("ko"), c("jl"), -8192.0, A.mult, 131072.0, A.add)
         cp(c("tf"), c("rqs"))
         conv_in("tf", "p5")
         cp(c("qi"), c("tr"))
@@ -394,51 +405,46 @@ def rank_program(g, core, T, topo):
 
     for t in range(RO):
         cp(c("ou"), c("oi"))
+        boost[0] = BOOST[0]
         for k in range(4):
             gat("s", c("wg", 1024 * k, 1024 * k + 1024), c("ww"), c("ou", 64 * k, 64 * k + 64))
+        boost[0] = 0.0
         ts(c("a2", 1, 256), c("ou", 0, 255), 2.0, A.mult, -1.0, A.add)
         cp(c("a2", 0, 256, 16), c("hv"))
         tt(c("t1"), c("a2"), c("p6", 0, 256), A.mult)
         ts(c("t2"), c("t1"), 4, A.arith_shift_right)
         tt(c("p7", 0, 256), c("t2"), c("p6", 0, 256), A.add)
-        ts(c("p37"), c("ou"), 37.0, A.mult, 77.0 * t - 37.0, A.add)
+        boost[0] = BOOST[4]
+        act(c("p37"), c("oi"), F.Identity, scale=37.0, bias=77.0 * t - 37.0)
+        boost[0] = 0.0
         tt(c("hi", 0, 256), c("p37"), c("p7", 0, 256), A.add)
         tt(pr("hi", 0, 8), pr("p37", 0), pr("p7", 1), A.add)
         tt(pr("hi", 1, 8), pr("p37", 1), pr("p7", 0), A.add)
         ts(c("hj"), c("hi"), 4095, A.bitwise_and)
         cp(c("hu"), c("hj"))
         for par in range(2):
-            ts(c("em", 128 * par, 128 * par + 128), pr("oi", par), 0.0, A.is_equal, 16384.0, A.mult)
+            act(c("em", 128 * par, 128 * par + 128), pr("oi", par), F.Relu, scale=-16384.0, bias=16384.0)
         o = c("p3", 0, 128)
         mms([(o, c("idb"), c("em", 128 * par, 128 * par + 128), par == 0, par == 1) for par in range(2)], o)
-        for s in range(2):
-            for k in range(4):
-                w, h = c("wg", 1024 * k, 1024 * k + 1024), c("hu", 256 * s + 64 * k, 256 * s + 64 * k + 64)
-                m = c("mn", 4096 * s + 1024 * k, 4096 * s + 1024 * k + 1024)
-                if (s, k) in VIA:
-                    xo = 1024 * VIA.index((s, k))
-                    gat("s", c("xo", xo, xo + 1024), c("xs"), h)
-                    for j in range(2):
-                        o = c(("p2", "p4")[j], 0, 512)
-                        mms([(o, c("idb"), w[5](512 * j, 512 * j + 512), True, False),
-                             (o, c("idn"), c("xo", xo + 512 * j, xo + 512 * j + 512), False, True)], o)
-                        act(m[5](512 * j, 512 * j + 512), o, F.Relu)
-                    continue
+        for (s, a, n, via) in PIECES:
+            w, h = c("wg", 16 * a, 16 * a + 16 * n), c("hu", 256 * s + a, 256 * s + a + n)
+            m = c("mn", 4096 * s + 16 * a, 4096 * s + 16 * a + 16 * n)
+            o = c("p%d" % s, a, a + n)
+            if not via:
                 run("v", [c("xs"), h, w], [m], lambda v, h=h, w=w, m=m: v.tensor_tensor(m[0], T.xs[:, 0:4096].indirect(h[0]), w[0], A.min),
-                    60 + GATHER * 1024)
-        def score(s, k):
-            o = c("p%d" % s, 64 * k, 64 * k + 64)
-            if (s, k) in VIA:
-                items = [(o, c("zs", 15 - i, 143 - i), c("wg", 1024 * k + i, 1024 * k + 1024, 16), i == 0, False) for i in range(16)]
-                a = 4096 * s + 1024 * k
-                mms(items + [(o, c("zn", 15 - i, 143 - i), c("mn", a + i, a + 1024, 16), False, i == 15) for i in range(16)], o)
-            else:
-                ext(o, "zs", "mn", 256 * s + 64 * k, 64)
-        for k in range(4):
-            score(0, k)
+                    60 + GATHER * 16 * n)
+                ext(o, "zs", "mn", 256 * s + a, n)
+                continue
+            x = c("xo", 0, 16 * n)
+            gat("s", x, c("xs"), h)
+            for j in range(n // 32):
+                d = c(("p2", "p4")[j], 0, 512)
+                mms([(d, c("idb"), w[5](512 * j, 512 * j + 512), True, False), (d, c("idn"), x[5](512 * j, 512 * j + 512), False, True)], d)
+                act(m[5](512 * j, 512 * j + 512), d, F.Relu)
+            items = [(o, c("zs", 15 - i, 143 - i), c("wg", 16 * a + i, 16 * (a + n), 16), i == 0, False) for i in range(16)]
+            b = 4096 * s + 16 * a
+            mms(items + [(o, c("zn", 15 - i, 143 - i), c("mn", b + i, b + 16 * n, 16), False, i == 15) for i in range(16)], o)
         act(c("m1s"), c("p0", 0, 256))
-        for k in range(4):
-            score(1, k)
         if t == 0:
             more_constants()
         tt(c("p7", 256, 512), c("p1", 0, 256), c("m1s"), A.subtract)
@@ -446,7 +452,9 @@ def rank_program(g, core, T, topo):
         tt(c("ds"), pr("p7", 0, 8), c("dob"), A.add)
         for par in range(2):
             tt(pr("sw", par), c("ds"), c("p3", 0, 128), A.is_gt)
-        dma("y", lane("cw", 2, 4096), c("sw"), "dsw")
+        for par in range(2):
+            ts(pr("swd", par), pr("sw", par), 16.0 - 32.0 * par, A.mult)
+        dma("y", lane("cw", 2, 4096), c("swd"), "dsw")
         tt(c("p7", 0, 256), c("p7", 256, 512), c("sw"), A.mult)
         tt(c("p7", 256, 512), c("p7", 0, 256), c("m1s"), A.add)
         cp(c("chi"), c("p7", 256, 512))
@@ -495,8 +503,8 @@ def rank_program(g, core, T, topo):
         tt(pr("c2l", 0), c("p7", 128, 256), pr("e1l", 0), A.add)
         tt(pr("c2l", 1), pr("e1l", 1), c("p7", 128, 256), A.subtract)
         ts(c("g32"), c("o2"), 16.0, A.mult)
-        tt(c("p7", 0, 256), c("p3", 256, 512), c("dq"), A.mult)
-        tt(c("qd"), c("p7", 0, 256), c("qi"), A.add)
+        tt(c("g32"), c("g32"), c("ko"), A.add)
+        tt(c("qd"), c("p3", 256, 512), c("qi"), A.add)
         cp(c("qdu"), c("qd"))
         ts(c("hq"), c("qd"), 4096 + 127, A.bitwise_and)
         ts(c("p7", 0, 256), c("hq"), float(16 * t), A.is_equal, -30000.0, A.mult)
@@ -507,14 +515,15 @@ def rank_program(g, core, T, topo):
         tt(c("mm"), mine, seq[0], A.max)
         for x in seq[1:]:
             tt(c("mm"), c("mm"), x, A.max)
+        boost[0] = BOOST[2]
         ts(c("m16"), c("mm"), -2040.0, A.add)
-        for r in range(16):
-            o = c("p4", r, 256, 16)
-            mms([(o, c("br", 128 * r, 128 * r + 128), c("m16"), True, True)], o)
+        mms([(c("p4", r, 256, 16), c("br", 128 * r, 128 * r + 128), c("m16"), True, True) for r in range(16)], c("p4", 0, 256))
         ts(c("mt"), c("p4", 0, 256), c("keq", 1, 2), A.mult)
         tt(c("mw", 1, 257), c("p4", 0, 256), c("mt"), A.subtract)
-        for k in range(3):
-            gat("s", c("mg", 1024 * k, 1024 * k + 1024), c("mw"), c("ou2", 64 * k, 64 * k + 64))
+        boost[0] = 0.0
+        for (q, a, n) in MPIECES:
+            if q == "s":
+                gat("s", c("mg", 16 * a, 16 * a + 16 * n), c("mw"), c("ou2", a, a + n))
         tt(c("s1"), c("mm"), c("ws"), A.add)
         ts(c("ui"), c("s1"), 255, A.bitwise_and)
         bc16(c("p6", 256, 512), c("mm"), "a16")
@@ -539,11 +548,7 @@ def rank_program(g, core, T, topo):
         tt(c("vb"), c("vb"), c("va"), A.mult)
         ts(c("uh"), c("vb"), 1024.0, A.add)
         ts(c("uc"), c("vb"), 1024.0, A.add)
-        for r in range(16):
-            o = c("p3", r, 256, 16)
-            mms([(o, c("br", 128 * r, 128 * r + 128), c("uh"), True, True)], o)
-        for k in range(3):
-            ext(c("p4", 64 * k, 64 * k + 64), "za", "mg", 64 * k, 64)
+        mms([(c("p3", r, 256, 16), c("br", 128 * r, 128 * r + 128), c("uh"), True, True) for r in range(16)], c("p3", 0, 256))
         cp(c("uu"), c("ui"))
         cp(c("ub"), c("p3", 0, 256))
         tt(c("um"), c("p3", 0, 256), c("lt"), A.add)
@@ -567,34 +572,41 @@ def rank_program(g, core, T, topo):
         run("v", [c("pv"), c("uou")], [c("qw")], lambda v: v.tensor_copy(T.qw[:, 0:512].indirect(T.uou[:, 0:16]), T.pv[:, 0:256]), 900)
         o = c("p5", 288, 304)
         mms([(o, c("zf", 15 - r, 143 - r), c("qw", 16 * r, 16 * r + 16), r == 0, r == 15) for r in range(16)], o)
-        gat("v", c("mg", 3072, 4096), c("mw"), c("ou2", 192, 256))
-        ext(c("p4", 192, 256), "za", "mg", 192, 64)
+        for (q, a, n) in MPIECES:
+            if q == "v":
+                gat("v", c("mg", 16 * a, 16 * a + 16 * n), c("mw"), c("ou2", a, a + n))
+            ext(c("p4", a, a + n), "za", "mg", a, n)
         sh = c("p6", 256, 512)
         tt(c("lv"), c("p4", 0, 256), c("c2l"), A.is_gt)
         tt(c("st"), c("p4", 0, 256), c("c2l"), A.is_le)
         scan(sh, c("rr"), c("lv"))
         tt(c("p7", 256, 512), c("g32"), sh, A.add)
         tt(c("yb"), c("p7", 256, 512), c("st"), A.mult)
+        boost[0] = BOOST[1]
         x_lists()
+        boost[0] = 0.0
         bc16(sh, c("le32"), "a17")
         tt(c("fe"), c("jl"), sh, A.is_equal)
+        tt(c("p7", 256, 512), c("jl"), sh, A.is_gt)
         for b in range(4):
             d = 1 << b
             y, m, to = k3("yb", d, 16), k3("p2", d, 16), k3("yb", 0, 16 - d)
             ts(k3("tb", d, 16), y, b, A.arith_shift_right, 1, A.bitwise_and)
             tt(m, k3("tb", d, 16), y, A.mult)
-            tt(y, y, m, A.subtract)
-            tt(to, to, m, A.add)
-        ts(c("yb"), c("yb"), 4, A.arith_shift_right)
+            tt(to, to, m, A.max)
+        ts(c("yb"), c("yb"), 4, A.arith_shift_right, 511, A.bitwise_and)
+        tt(c("yb"), c("yb"), c("p7", 256, 512), A.mult)
         cp(c("ap", 0, 16), c("p5", 288, 304))
         bc16(sh, c("ap", 0, 16), "a16")
         tt(c("p7", 0, 256), c("fe"), sh, A.mult)
         tt(c("oi"), c("yb"), c("p7", 0, 256), A.add)
+        boost[0] = BOOST[3]
         for k in range(4):
             x_gather("v" if t == RO - 1 and k == 3 else "s", k)
             x_ext(k)
         len_gather()
         len_ext()
+        boost[0] = 0.0
     ts(c("tf"), c("oi"), 0.0, A.is_equal, 257.0, A.mult)
     ts(c("tg"), c("oi"), -1.0, A.add)
     tt(c("tr"), c("tf"), c("tg"), A.add)
@@ -607,7 +619,7 @@ def rank_program(g, core, T, topo):
     conv_out("tg", "p1")
     dma("y", T.yq[:, :], c("tg"), "dyq")
     for i in schedule():
-        q, rd, wr, call, hold, sem, inc, lag = ops[i]
+        q, rd, wr, call, hold, sem, inc = ops[i][:7]
         if call is None:
             cnt[sem] += inc
             note(q, [], wr[:1], sem, cnt[sem])

@@ -14,14 +14,14 @@ for _n, _w, _d in [
     ("qw", 512, "bfloat16"),
     ("roc", 256, "int32"), ("rqs", 256, "int32"), ("rth", 1, "int32"),
     ("zs", 144, "bfloat16"), ("za", 144, "bfloat16"), ("zf", 144, "bfloat16"), ("zw", 144, "bfloat16"),
-    ("br", 2048, "float16"), ("e0", 160, "float32"), ("e1", 160, "float32"),
+    ("br", 2048, "float16"), ("e0", 160, "float16"), ("e1", 160, "float16"),
     ("idb", 128, "bfloat16"),
     ("ip", 1, "int32"), ("ki", 1, "int32"), ("cf", 16, "float32"), ("keq", 16, "float32"),
     ("ci", 256, "float32"), ("c16", 16, "float32"), ("ni", 256, "int32"), ("zn", 144, "bfloat16"), ("idn", 128, "bfloat16"), ("bo", 128, "bfloat16"),
     ("lt", 256, "float32"), ("um", 256, "float32"), ("ub", 256, "bfloat16"), ("eqb", 2176, "bfloat16"), ("lz", 256, "bfloat16"), ("xo", 2048, "bfloat16"),
     ("na", 256, "int32"), ("thl", 1024, "float32"), ("jl", 256, "float32"), ("rr", 256, "float32"),
     ("pll", 16, "float32"), ("pv", 256, "bfloat16"), ("ws", 16, "float32"),
-    ("hv", 16, "float32"), ("tf", 256, "float32"), ("tg", 256, "float32"), ("rt", 256, "float32"), ("of", 256, "float32"),
+    ("hv", 16, "float32"), ("tf", 256, "float32"), ("tg", 256, "float32"), ("rt", 256, "float16"), ("m1o", 256, "float32"), ("of", 256, "float32"),
     ("ou", 256, "uint16"), ("ou2", 256, "uint16"),
     ("qi", 256, "int32"), ("qd", 256, "int32"), ("qu", 256, "uint16"), ("qdu", 256, "uint16"), ("ko", 256, "float32"),
     ("a2", 256, "float32"), ("t1", 256, "int32"), ("t2", 256, "int32"), ("hj", 512, "int32"),
@@ -32,14 +32,15 @@ for _n, _w, _d in [
     ("s1", 16, "int32"), ("ui", 16, "int32"), ("a16", 256, "float32"), ("a17", 256, "float32"), ("f16", 16, "float32"),
     ("va", 16, "float32"), ("vb", 16, "float32"), ("uc", 16, "float32"), ("uh", 16, "float16"), ("tk", 512, "float32"), ("wi", 16, "float32"), ("uo", 16, "float32"), ("uou", 16, "uint16"), ("uu", 16, "uint16"),
     ("lv", 256, "float32"), ("st", 256, "float32"), ("lvb", 256, "bfloat16"), ("xl", 256, "bfloat16"), ("le", 16, "bfloat16"),
-    ("ap", 64, "float32"), ("sl", 64, "float32"), ("land", 256, "float32"), ("bs", 64, "float32"),
+    ("ap", 64, "float32"), ("sl", 64, "float32"),
+    ("land", 256, "float32"), ("bs", 64, "float32"),
 ]:
     SCRATCH[_n] = ("sbuf", [128, _w], _d)
 for _n, _r, _w, _d in [
     ("yb", 16, 16, "int32"), ("tb", 16, 16, "int32"), ("tr", 8, 32, "float32"), ("oi", 8, 32, "float32"), ("swd", 8, 32, "bfloat16"), ("o2", 8, 32, "int32"),
     ("hi", 16, 32, "int32"), ("p37", 8, 32, "float32"), ("m1s", 8, 32, "float32"), ("sw", 8, 32, "bfloat16"), ("ccs", 8, 32, "float32"),
     ("e1l", 8, 32, "float32"), ("c2l", 8, 32, "float32"), ("dob", 8, 16, "float32"), ("ds", 8, 16, "float32"),
-    ("t8", 16, 8, "float32"), ("t8b", 16, 8, "float32"), ("t4", 16, 4, "float32"), ("t2x", 16, 2, "float32"), ("jv", 16, 16, "float32"),
+    ("t8", 16, 8, "float32"), ("t4", 16, 4, "float32"), ("t2x", 16, 2, "float32"), ("jv", 16, 16, "float32"),
 ]:
     SCRATCH[_n] = ("sbuf", [128, _r, _w], _d)
 for _n in ("p1", "p3", "p4", "p5", "p6"):
@@ -51,9 +52,9 @@ SEMAPHORES = ["sv", "ss", "st", "sg", "snt", "arr0", "arr1", "arr2", "arr3", "dx
               "dhi", "dlo", "dsw", "dxl", "dle", "dyo", "dyq"]
 QSEM = {"v": "sv", "s": "ss", "t": "st", "g": "sg", "n": ""}
 LANES = {"cw": ["cw_0", "cw_1", "cw_2"], "xw": ["xw_0"], "lw": ["lw_0"]}
-CY, WAKE, GATHER, EARLY, SPLIT = 0.00083, 0.15, 1.4, 0.0, True
+CY, WAKE, GATHER, EARLY, SPLIT = 0.00083, 0.17, 1.6, 0.06, True
 PIECES = [(0, 0, 64, 0), (0, 64, 64, 0), (0, 128, 64, 0), (0, 192, 64, 0), (1, 192, 64, 1), (1, 0, 64, 0), (1, 64, 64, 0), (1, 128, 64, 0)]
-BOOST = [0.0, 3.0, 6.0, 0.0, 9.0]
+BOOST = [0.0, 3.0, 6.0, 0.0, 9.0, 0.0, 0.0, 0.0]
 MPIECES = [("s", 0, 64), ("s", 64, 64), ("s", 128, 64), ("v", 192, 64)]
 
 
@@ -291,13 +292,13 @@ def rank_program(g, core, T, topo):
 
     def swap16(psname):
         for de in range(2):
-            cp(c("rt", 128 * de, 128 * de + 128), pr("tr", de))
+            ts(c("rt", 128 * de, 128 * de + 128), pr("tr", de), -2048.0, A.add)
         for al in range(2):
             o = c(psname, 128 * al, 128 * al + 128)
             mms([(o, c("e%d" % al, 16 + 16 * (al - de), 144 + 16 * (al - de)), c("rt", 128 * de, 128 * de + 128), de == 0, de == 1)
                  for de in range(2)], o)
         for al in range(2):
-            cp(pr("tr", al), c(psname, 128 * al, 128 * al + 128))
+            ts(pr("tr", al), c(psname, 128 * al, 128 * al + 128), 2048.0, A.add)
 
     def flip(a):
         return (T.tr[:, a, :], "tr", 32 * a, 32 * a + 32)
@@ -337,7 +338,7 @@ def rank_program(g, core, T, topo):
         ts(c("zw"), c("ci", 0, 144), col(2), A.is_equal, col(10), A.mult)
         o = c("p5", 0, 16)
         mms([(o, c("zw", 15 - i, 143 - i), c("ww", 1 + i, 257, 16), i == 0, i == 15) for i in range(16)], o)
-        cp(c("ws"), o)
+        ts(c("ws"), o, 2040.0, A.add)
         for n in ("mw", "lw", "a16", "a17"):
             fill(c(n), 0.0)
         ts(c("cw", 4096, 4097), c("keq", 0, 1), NOB, A.mult)
@@ -348,11 +349,10 @@ def rank_program(g, core, T, topo):
         ts(c("ni"), c("ci"), col(4), A.add)
         ts(c("na"), c("ni"), 127, A.bitwise_and)
         cp(col(11), c("rth"))
-        ts(col(12), c("rth"), -2040.0, A.add)
         for t in range(RO):
             x = c("thl", 256 * t, 256 * t + 256)
             ts(x, c("na"), float(16 * t), A.is_equal, -30000.0, A.mult)
-            act(x, x, F.Identity, bias=col(12), scale=1.0)
+            act(x, x, F.Identity, bias=col(11), scale=1.0)
         ts(c("rr"), c("jl"), 16.0, A.is_lt)
         ts(c("uo"), c("c16"), 16.0, A.mult, col(1), A.add)
         ts(c("pll"), c("uo"), 256.0, A.add)
@@ -384,11 +384,12 @@ def rank_program(g, core, T, topo):
         tt(c("qi"), q2, c("p7", 0, 256), A.add)
 
     def x_lists():
-        ts(c("lvb"), c("lv"), 4608.0, A.mult)
+        for a in (0, 128):
+            act(c("lvb", a, a + 128), c("lv", a, a + 128), F.Copy, scale=4608.0)
         tt(c("xl"), c("lvb"), c("p6", 256, 512), A.subtract)
         dma("y", lane("xw", 0, 4096), c("xl"), "dxl")
         cp(c("le32"), c("p6", 256 + 15, 512, 16))
-        cp(c("le"), c("le32"))
+        act(c("le"), c("le32"))
         dma("y", lane("lw", 0, 256), c("le"), "dle")
 
     def x_gather(q, k):
@@ -436,6 +437,7 @@ def rank_program(g, core, T, topo):
                 ext(o, "zs", "mn", 256 * s + a, n)
                 continue
             x = c("xo", 0, 16 * n)
+            boost[0] = BOOST[7]
             gat("s", x, c("xs"), h)
             for j in range(n // 32):
                 d = c(("p2", "p4")[j], 0, 512)
@@ -444,7 +446,9 @@ def rank_program(g, core, T, topo):
             items = [(o, c("zs", 15 - i, 143 - i), c("wg", 16 * a + i, 16 * (a + n), 16), i == 0, False) for i in range(16)]
             b = 4096 * s + 16 * a
             mms(items + [(o, c("zn", 15 - i, 143 - i), c("mn", b + i, b + 16 * n, 16), False, i == 15) for i in range(16)], o)
+            boost[0] = 0.0
         act(c("m1s"), c("p0", 0, 256))
+        act(c("m1o"), c("m1s"), F.Identity, bias=-2040.0, scale=1.0)
         if t == 0:
             more_constants()
         tt(c("p7", 256, 512), c("p1", 0, 256), c("m1s"), A.subtract)
@@ -456,7 +460,7 @@ def rank_program(g, core, T, topo):
             ts(pr("swd", par), pr("sw", par), 16.0 - 32.0 * par, A.mult)
         dma("y", lane("cw", 2, 4096), c("swd"), "dsw")
         tt(c("p7", 0, 256), c("p7", 256, 512), c("sw"), A.mult)
-        tt(c("p7", 256, 512), c("p7", 0, 256), c("m1s"), A.add)
+        tt(c("p7", 256, 512), c("p7", 0, 256), c("m1o"), A.add)
         cp(c("chi"), c("p7", 256, 512))
         dma("y", lane("cw", 0, 4096), c("chi"), "dhi")
         tt(c("clo"), c("p7", 256, 512), c("chi"), A.subtract)
@@ -466,14 +470,15 @@ def rank_program(g, core, T, topo):
             q_lists()
         for k in (0, 2, 1, 3):
             gat("v" if k < 2 else "s", c("cg", 1024 * k, 1024 * k + 1024), c("cw"), c("qu", 64 * k, 64 * k + 64))
-            ext(c("p0", 256 + 64 * k, 256 + 64 * k + 64), "za", "cg", 64 * k, 64)
+            bank = ("p4", "p5", "p1", "p0")[k]
+            ext(c(bank, 0, 64), "za", "cg", 64 * k, 64)
+            for j in range(4):
+                i, o = c(bank, 16 * j, 16 * j + 16), c("bs", 16 * t + 4 * k + j, 16 * t + 4 * k + j + 1)
+                i2 = T.p0[:, j, :] if bank == "p0" else i[0]
+                run("v", [i], [o], lambda v, i2=i2, o=o: v.tensor_reduce(o[0], i2, AxisListType.X, A.max))
+            act(c("cs", 64 * k, 64 * k + 64), c(bank, 0, 64), F.Identity, bias=col(11), scale=1.0)
         ext(c("p3", 256, 512), "zf", "cg", 0, 256)
-        cp(c("t8"), k3("p0", 8, 16, 16, 32))
-        tt(c("t8b"), k3("p0", 0, 8, 16, 32), c("t8"), A.max)
-        tt(c("t4"), k3("t8b", 0, 4), k3("t8b", 4, 8), A.max)
-        tt(c("t2x"), k3("t4", 0, 2), k3("t4", 2, 4), A.max)
         mine = c("bs", 16 * t, 16 * t + 16)
-        tt(mine, k1("t2x", 0), k1("t2x", 1), A.max)
         others = [d for d in T.cores if d != core]
         mask = 0xFFFFFFFF
         for d in others:
@@ -489,7 +494,6 @@ def rank_program(g, core, T, topo):
         wire = (None, "wire", t, t + 1)
         add("g", [mine], [wire], lambda e, s, send=send: e.remote_dma_fused([send], local_sem=s), 0.5, "snt", eng, 0.0)
         add("n", [], [c("land", 64 * t, 64 * t + 64), wire], None, 0.0, "arr%d" % t, eng * (n_ranks - 1), 4.0)
-        act(c("cs"), c("p0", 256, 512), F.Identity, bias=col(11), scale=1.0)
         fill(c("qw"), 0.0)
         tt(c("p7", 0, 128), pr("oi", 1), pr("oi", 0), A.subtract)
         tt(c("p7", 128, 256), c("p7", 0, 128), pr("sw", 0), A.mult)
@@ -512,11 +516,12 @@ def rank_program(g, core, T, topo):
         lands = [c("land", 64 * t + 16 * r, 64 * t + 16 * r + 16) for r in range(n_ranks)]
         lower, higher = lands[:rank], lands[rank + 1:]
         seq = lower + higher
-        tt(c("mm"), mine, seq[0], A.max)
-        for x in seq[1:]:
-            tt(c("mm"), c("mm"), x, A.max)
         boost[0] = BOOST[2]
-        ts(c("m16"), c("mm"), -2040.0, A.add)
+        m2 = [c("ap", 0, 16), c("ap", 16, 32)]
+        tt(m2[0], mine, seq[0], A.max)
+        tt(m2[1], seq[1], seq[2], A.max)
+        tt(c("m16"), m2[0], m2[1], A.max)
+        tt(c("mm"), m2[0], m2[1], A.max)
         mms([(c("p4", r, 256, 16), c("br", 128 * r, 128 * r + 128), c("m16"), True, True) for r in range(16)], c("p4", 0, 256))
         ts(c("mt"), c("p4", 0, 256), c("keq", 1, 2), A.mult)
         tt(c("mw", 1, 257), c("p4", 0, 256), c("mt"), A.subtract)
@@ -563,23 +568,28 @@ def rank_program(g, core, T, topo):
         for a, b in ((0, 6), (6, 11), (11, 16)):
             mms([(los[z] + (z == 0, z == 15)) for z in range(a, b)], c("p1", 0, 256))
         ts(c("lz"), c("p1", 0, 256), 0.0, A.is_equal)
-        ext(c("p5", 272, 288), "zf", "lz", 0, 16)
-        tt(c("wi"), c("va"), c("p5", 272, 288), A.mult)
+        ext(c("p1", 272, 288), "zf", "lz", 0, 16)
+        tt(c("wi"), c("va"), c("p1", 272, 288), A.mult)
         tt(c("uo"), c("uc"), c("pll"), A.subtract)
         tt(c("uo"), c("uo"), c("wi"), A.mult)
         tt(c("uo"), c("uo"), c("pll"), A.add)
         cp(c("uou"), c("uo"))
         run("v", [c("pv"), c("uou")], [c("qw")], lambda v: v.tensor_copy(T.qw[:, 0:512].indirect(T.uou[:, 0:16]), T.pv[:, 0:256]), 900)
-        o = c("p5", 288, 304)
+        o = c("p1", 288, 304)
         mms([(o, c("zf", 15 - r, 143 - r), c("qw", 16 * r, 16 * r + 16), r == 0, r == 15) for r in range(16)], o)
         for (q, a, n) in MPIECES:
             if q == "v":
                 gat("v", c("mg", 16 * a, 16 * a + 16 * n), c("mw"), c("ou2", a, a + n))
             ext(c("p4", a, a + n), "za", "mg", a, n)
         sh = c("p6", 256, 512)
+        boost[0] = BOOST[5]
         tt(c("lv"), c("p4", 0, 256), c("c2l"), A.is_gt)
-        tt(c("st"), c("p4", 0, 256), c("c2l"), A.is_le)
+        boost[0] = BOOST[6]
+        for a in (0, 128):
+            act(c("st", a, a + 128), c("lv", a, a + 128), F.Identity, scale=-1.0, bias=1.0)
+        boost[0] = BOOST[5]
         scan(sh, c("rr"), c("lv"))
+        boost[0] = 0.0
         tt(c("p7", 256, 512), c("g32"), sh, A.add)
         tt(c("yb"), c("p7", 256, 512), c("st"), A.mult)
         boost[0] = BOOST[1]
@@ -596,8 +606,7 @@ def rank_program(g, core, T, topo):
             tt(to, to, m, A.max)
         ts(c("yb"), c("yb"), 4, A.arith_shift_right, 511, A.bitwise_and)
         tt(c("yb"), c("yb"), c("p7", 256, 512), A.mult)
-        cp(c("ap", 0, 16), c("p5", 288, 304))
-        bc16(sh, c("ap", 0, 16), "a16")
+        bc16(sh, c("p1", 288, 304), "a16")
         tt(c("p7", 0, 256), c("fe"), sh, A.mult)
         tt(c("oi"), c("yb"), c("p7", 0, 256), A.add)
         boost[0] = BOOST[3]
@@ -607,12 +616,12 @@ def rank_program(g, core, T, topo):
         len_gather()
         len_ext()
         boost[0] = 0.0
-    ts(c("tf"), c("oi"), 0.0, A.is_equal, 257.0, A.mult)
-    ts(c("tg"), c("oi"), -1.0, A.add)
+    act(c("tf"), c("oi"), F.Relu, scale=-257.0, bias=257.0)
+    act(c("tg"), c("oi"), F.Identity, scale=1.0, bias=-1.0)
     tt(c("tr"), c("tf"), c("tg"), A.add)
     conv_out("of", "p1")
     for q in range(16):
-        cp(c("um", q, 256, 16), c("of", 16 * q, 16 * q + 16))
+        act(c("um", q, 256, 16), c("of", 16 * q, 16 * q + 16))
     dma("y", T.yoc[:, :], c("um"), "dyo")
     q_update()
     cp(c("tr"), c("qi"))

from concourse.bass import DstId, RemoteDMATransfer
from concourse.mybir import AluOpType, AxisListType, ActivationFunctionType

A = AluOpType
F = ActivationFunctionType
RO = 4
NOB = -29952.0

SCRATCH = {}
for _n, _w, _d in [
    ("xs", 4096, "bfloat16"), ("ww", 272, "bfloat16"), ("wg", 4096, "bfloat16"), ("mn", 8192, "bfloat16"),
    ("cw", 4112, "bfloat16"), ("cg", 4096, "bfloat16"), ("xw", 4112, "bfloat16"), ("xg", 4096, "bfloat16"),
    ("mw", 272, "bfloat16"), ("mg", 4096, "bfloat16"), ("lw", 256, "bfloat16"), ("lg", 256, "bfloat16"),
    ("qw", 512, "bfloat16"),
    ("roc", 256, "int32"), ("rqs", 256, "int32"), ("rth", 1, "int32"),
    ("zs", 144, "bfloat16"), ("za", 144, "bfloat16"), ("zf", 144, "bfloat16"), ("zw", 144, "bfloat16"),
    ("br", 2048, "float16"), ("e0", 160, "float16"), ("e1", 160, "float16"),
    ("idb", 128, "bfloat16"),
    ("ip", 1, "int32"), ("ki", 1, "int32"), ("cf", 16, "float32"), ("keq", 16, "float32"),
    ("ci", 256, "float32"), ("c16", 16, "float32"), ("ni", 256, "int32"), ("zn", 144, "bfloat16"), ("idn", 128, "bfloat16"), ("bo", 128, "bfloat16"),
    ("lt", 256, "float32"), ("um", 256, "float32"), ("ub", 256, "bfloat16"), ("eqb", 2176, "bfloat16"), ("lz", 256, "bfloat16"), ("xo", 2048, "bfloat16"),
    ("na", 256, "int32"), ("thl", 1024, "float32"), ("jl", 256, "float32"), ("rr", 256, "float32"),
    ("pll", 16, "float32"), ("pv", 256, "bfloat16"), ("ws", 16, "float32"),
    ("hv", 16, "float32"), ("tf", 256, "float32"), ("tg", 256, "float32"), ("rt", 256, "float16"), ("m1o", 256, "float32"), ("of", 256, "float32"),
    ("ou", 256, "uint16"), ("ou2", 256, "uint16"),
    ("qi", 256, "int32"), ("qd", 256, "int32"), ("qu", 256, "uint16"), ("qdu", 256, "uint16"), ("ko", 256, "float32"),
    ("a2", 256, "float32"), ("t1", 256, "int32"), ("t2", 256, "int32"), ("hj", 512, "int32"),
    ("hu", 512, "uint16"), ("em", 256, "bfloat16"),
    ("chi", 256, "bfloat16"), ("clo", 256, "bfloat16"), ("cs", 256, "float32"), ("cx", 256, "float32"),
    ("g32", 256, "float32"), ("fe", 256, "float32"), ("le32", 16, "float32"), ("hq", 256, "int32"),
    ("mm", 16, "float32"), ("m16", 16, "float16"), ("mt", 256, "bfloat16"),
    ("s1", 16, "int32"), ("ui", 16, "int32"), ("a16", 256, "float32"), ("a17", 256, "float32"), ("f16", 16, "float32"),
    ("va", 16, "float32"), ("vb", 16, "float32"), ("uc", 16, "float32"), ("uh", 16, "float16"), ("tk", 512, "float32"), ("wi", 16, "float32"), ("uo", 16, "float32"), ("uou", 16, "uint16"), ("uu", 16, "uint16"),
    ("lv", 256, "float32"), ("st", 256, "float32"), ("lvb", 256, "bfloat16"), ("xl", 256, "bfloat16"), ("le", 16, "bfloat16"),
    ("ap", 64, "float32"), ("sl", 64, "float32"),
    ("land", 256, "float32"), ("bs", 64, "float32"),
]:
    SCRATCH[_n] = ("sbuf", [128, _w], _d)
for _n, _r, _w, _d in [
    ("yb", 16, 16, "int32"), ("tb", 16, 16, "int32"), ("tr", 8, 32, "float32"), ("oi", 8, 32, "float32"), ("swd", 8, 32, "bfloat16"), ("o2", 8, 32, "int32"),
    ("hi", 16, 32, "int32"), ("p37", 8, 32, "float32"), ("m1s", 8, 32, "float32"), ("sw", 8, 32, "bfloat16"), ("ccs", 8, 32, "float32"),
    ("e1l", 8, 32, "float32"), ("c2l", 8, 32, "float32"), ("dob", 8, 16, "float32"), ("ds", 8, 16, "float32"),
    ("t8", 16, 8, "float32"), ("t4", 16, 4, "float32"), ("t2x", 16, 2, "float32"), ("jv", 16, 16, "float32"),
]:
    SCRATCH[_n] = ("sbuf", [128, _r, _w], _d)
for _n in ("p1", "p3", "p4", "p5", "p6"):
    SCRATCH[_n] = ("psum", [128, 512], "float32")
SCRATCH["p0"] = ("psum", [128, 32, 16], "float32")
SCRATCH["p2"] = ("psum", [128, 16, 32], "float32")
SCRATCH["p7"] = ("psum", [128, 16, 32], "float32")
SEMAPHORES = ["sv", "ss", "st", "sg", "snt", "arr0", "arr1", "arr2", "arr3", "dx", "dw", "doc", "dqs", "dth",
              "dhi", "dlo", "dsw", "dxl", "dle", "dyo", "dyq"]
QSEM = {"v": "sv", "s": "ss", "t": "st", "g": "sg", "n": ""}
LANES = {"cw": ["cw_0", "cw_1", "cw_2"], "xw": ["xw_0"], "lw": ["lw_0"]}
CY, WAKE, GATHER, EARLY, SPLIT = 0.00083, 0.17, 1.6, 0.06, True
PIECES = [(0, 0, 64, 0), (0, 64, 64, 0), (0, 128, 64, 0), (0, 192, 64, 0), (1, 192, 64, 1), (1, 0, 64, 0), (1, 64, 64, 0), (1, 128, 64, 0)]
BOOST = [0.0, 3.0, 6.0, 0.0, 9.0, 0.0, 0.0, 0.0]
MPIECES = [("s", 0, 64), ("s", 64, 64), ("s", 128, 64), ("v", 192, 64)]


def rank_program(g, core, T, topo):
    rank = T.rank_of(core)
    if rank is None:
        return
    n_ranks = len(T.cores)
    queues = {"v": g.vector, "s": g.scalar, "t": g.tensor, "y": g.sync, "g": g}
    cnt = dict((s, 0) for s in SEMAPHORES)
    known = dict((q, {}) for q in queues)
    log = dict((n, []) for n in list(SCRATCH) + ["wire"] + sum(LANES.values(), []))
    psum = set(n for n in SCRATCH if SCRATCH[n][0] == "psum")

    def c(name, a=0, b=None, step=1):
        shp = SCRATCH[name][1]
        if len(shp) == 3:
            w = shp[2]
            if b is None:
                b = shp[1] * w
            return (T[name][:, a // w:b // w, :], name, a, b, b - a, lambda x, y: c(name, a + x, a + y), w)
        if b is None:
            b = shp[1]
        return (T[name][:, a:b:step] if step > 1 else T[name][:, a:b], name, a, b, (b - a + step - 1) // step,
                lambda x, y: c(name, a + x * step, min(b, a + y * step), step), 1, step)

    def k3(name, lo, hi, r0=0, r1=None):
        shp = SCRATCH[name][1]
        if r1 is None:
            r1 = shp[1]
        w = hi - lo
        return (T[name][:, r0:r1, lo:hi], name, r0 * shp[2], r1 * shp[2], (r1 - r0) * w,
                lambda x, y: k3(name, lo, hi, r0 + x // w, r0 + y // w), w)

    def k1(name, j):
        shp = SCRATCH[name][1]
        return (T[name][:, :, j], name, 0, shp[1] * shp[2], shp[1], None)

    def pr(name, par, r0=0):
        return k3(name, 16 * par, 16 * par + 16, r0, r0 + 8)

    def region(x, isw):
        return (x[1], x[2], x[3], x[7] if len(x) > 7 else 1, isw)

    def meet(x, e, q):
        name, lo, hi, st, w = x
        if name in psum and e[4] != q:
            return True
        return e[0] < hi and lo < e[1] and (w or e[3]) and not (st > 1 and st == e[2] and (lo - e[0]) % st)

    def covered(x, e, q):
        name, lo, hi, st, w = x
        return lo <= e[0] and e[1] <= hi and (st == 1 or (st == e[2] and lo == e[0])) and (w or not e[3]) and (e[4] == q or (w and name not in psum))

    def order(q, rd, wr):
        need = {}
        for x in [region(r, False) for r in rd] + [region(w, True) for w in wr]:
            for e in log[x[0]]:
                if meet(x, e, q):
                    sem, val = e[5:]
                    if need.get(sem, 0) < val:
                        need[sem] = val
        for sem in sorted(need):
            if known[q].get(sem, 0) < need[sem]:
                queues[q].wait_ge(T.sem[sem], need[sem])
                known[q][sem] = need[sem]

    def note(q, rd, wr, sem, val):
        for x in [region(r, False) for r in rd] + [region(w, True) for w in wr]:
            log[x[0]] = [e for e in log[x[0]] if not (covered(x, e, q) and (x[4] or e[5] == sem))]
            log[x[0]].append(x[1:] + (q, sem, val))

    ops, boost = [], [0.0]

    def add(q, rd, wr, call, hold, sem=None, inc=1, lag=0.0):
        ops.append((q, rd, wr, call, hold, sem or QSEM[q], inc, lag, boost[0]))

    def run(q, rd, wr, call, n=64):
        add(q, rd, wr, lambda e, s: call(e).then_inc(s, 1), CY * max(64, n))

    def cols(*xs):
        return [x for x in xs if isinstance(x, tuple)]

    def raw(x):
        return x[0] if isinstance(x, tuple) else x

    def size(x):
        return 2 if SCRATCH[x[1]][2] in ("bfloat16", "uint16", "float16") else 4

    def parts(out, n, *xs):
        h = out[4] // 2
        if n < 128 or out[4] % 2 or not SPLIT or any(x[5] is None or h % x[6] for x in (out,) + xs):
            return [(out,) + xs]
        return [tuple(x[5](a, a + h) for x in (out,) + xs) for a in (0, h)]

    def tt(out, a, b, op):
        n = out[4] * (1 if a[1] in psum or b[1] in psum else 2)
        for o, x, y in parts(out, n, a, b):
            run("v", [x, y], [o], lambda v, o=o, x=x, y=y: v.tensor_tensor(o[0], x[0], y[0], op), n * o[4] // out[4])

    def ts(out, a, s1, op0, s2=None, op1=None):
        n = out[4] if size(out) + size(a) > 4 else out[4] // 2
        for o, x in parts(out, n, a):
            if op1 is None:
                run("v", [x] + cols(s1), [o], lambda v, o=o, x=x: v.tensor_scalar(o[0], x[0], raw(s1), None, op0), n * o[4] // out[4])
            else:
                run("v", [x] + cols(s1, s2), [o], lambda v, o=o, x=x: v.tensor_scalar(o[0], x[0], raw(s1), raw(s2), op0, op1), n * o[4] // out[4])

    def cp(out, a):
        n = out[4] if size(out) + size(a) > 4 else out[4] // 2
        for o, x in parts(out, n, a):
            run("v", [x], [o], lambda v, o=o, x=x: v.tensor_copy(o[0], x[0]), n * o[4] // out[4])

    def fill(out, x):
        run("v", [], [out], lambda v: v.memset(out[0], x), out[4] // 2)

    def scan(out, d0, d1):
        for o, x, y in parts(out, out[4], d0, d1):
            run("v", [x, y], [o], lambda v, o=o, x=x, y=y: v.tensor_tensor_scan(o[0], x[0], y[0], 0.0, A.mult, A.add), o[4])

    def act(out, a, func=F.Copy, **kw):
        k2 = dict((k, raw(kw[k])) for k in kw)
        run("s", [a] + cols(*kw.values()), [out], lambda s: s.activation(out[0], a[0], func, **k2), 60 + out[4])

    def gat(q, out, win, off):
        rd = [win, off] + [(None, x, 0, 9999) for x in LANES.get(win[1], [])]
        if q == "v":
            run("v", rd, [out], lambda v: v.tensor_copy(out[0], win[0].indirect(off[0])), 60 + GATHER * out[4])
        else:
            run("s", rd, [out], lambda s: s.activation(out[0], win[0].indirect(off[0]), F.Copy), 80 + GATHER * out[4])

    def mms(items, out):
        rd = []
        for it in items:
            rd += [it[1], it[2]]

        def call(e, s):
            for (o, l, r, a, b) in items:
                i = e.matmul(o[0], l[0], r[0], a, b)
            i.then_inc(s, 1)
        add("t", rd, [out], call, CY * sum(max(64, r[4]) * (4 if size(r) == 4 else 1) for (_, _, r, _, _) in items))

    def schedule():
        n = len(ops)
        pred, succ, seen = [], [[] for _ in range(n)], dict((b, []) for b in log)
        for i, (q, rd, wr) in enumerate(op[:3] for op in ops):
            p = set()
            accs = [region(r, False) for r in rd] + [region(w, True) for w in wr]
            for x in accs:
                p.update(e[5] for e in seen[x[0]] if meet(x, e, q))
            for x in accs:
                seen[x[0]] = [e for e in seen[x[0]] if not (x[4] and covered(x, e, q))]
                seen[x[0]].append(x[1:] + (q, i))
            pred.append(p)
            for j in p:
                succ[j].append(i)
        way = [0.0] * n
        for i in range(n - 1, -1, -1):
            way[i] = ops[i][4] + ops[i][7] + max([0.0] + [way[j] + WAKE for j in succ[i]])
        left = [len(p) for p in pred]
        ready = [0.0] * n
        cand = set(i for i in range(n) if left[i] == 0)
        free, seq = {}, []
        while cand:
            first = min(max(free.get(ops[i][0], 0.0), ready[i]) for i in cand)
            now = [i for i in cand if max(free.get(ops[i][0], 0.0), ready[i]) <= first + EARLY]
            best = max(now, key=lambda i: (way[i] + ops[i][8], -i))
            cand.discard(best)
            q, hold, lag = ops[best][0], ops[best][4], ops[best][7]
            start = max(free.get(q, 0.0), ready[best])
            free[q] = start + hold
            seq.append(best)
            for j in succ[best]:
                ready[j] = max(ready[j], start + hold + lag + WAKE)
                left[j] -= 1
                if left[j] == 0:
                    cand.add(j)
        return seq

    def ext(out, z, name, c0, n):
        mms([(out, c(z, 15 - i, 143 - i), c(name, 16 * c0 + i, 16 * (c0 + n), 16), i == 0, i == 15) for i in range(16)], out)

    def dma(q, out, in_, sem):
        rd = cols(in_)
        wr = cols(out)
        if wr and wr[0][1] in log and wr[0][1] not in SCRATCH:
            rd = rd + [(None, wr[0][1][:-2], wr[0][2], wr[0][3])]
        add(q, rd, wr, lambda e, s: e.dma_start(raw(out), raw(in_)).then_inc(s, 16), 0.1, sem, 16, 2.0)

    def lane(name, f, w):
        return (T[name][f::16, 0:w], "%s_%d" % (name, f), 0, w, 0, None)

    dma("y", c("roc"), T.oc[:, :], "doc")
    dma("y", c("rqs"), T.qs[:, :], "dqs")
    fill(c("ww"), 0.0)
    dma("s", c("rth"), T.th[:, :], "dth")
    dma("s", c("xs"), T.x[:, :], "dx")
    dma("y", c("ww", 1, 257), T.want[:, :], "dw")

    def iota(out, pattern, base, cm):
        if SCRATCH[out[1]][2] == "int32":
            run("g", [], [out], lambda e: e.iota(out[0], pattern, base, cm))
        else:
            run("g", [], [out], lambda e: e.iota(out[0], pattern, base, cm, allow_small_or_imprecise_dtypes=True), 160 + 2 * out[4])

    def col(j):
        return c("cf", j, j + 1)

    iota(c("ip"), [[0, 1]], 0, 1)
    iota(c("ci"), [[1, 256]], 0, 0)
    iota(c("c16"), [[1, 16]], 0, 0)
    iota(c("jl"), [[0, 16], [-1, 16]], 16, 0)
    iota(c("um", 0, 128), [[16, 8], [0, 16]], 0, 0)
    iota(c("lt"), [[0, 16], [1, 16]], 0, 0)
    iota(c("cw"), [[0, 4112]], 0, 0)
    iota(c("pv"), [[1, 256]], 1, 0)
    iota(c("xw"), [[0, 4112]], 0, 0)
    ts(c("ki"), c("ip"), 15, A.bitwise_and)
    tt(c("s1", 1, 2), c("ip"), c("ki"), A.subtract)
    cp(col(0), c("ip"))
    cp(col(1), c("ki"))
    ts(col(2), c("s1", 1, 2), 15.0, A.add)
    ts(col(3), c("ip"), 16.0, A.add)
    ts(col(4), c("ki"), 256.0, A.mult)
    ts(col(5), c("ki"), 32.0, A.mult, 1.0, A.add)
    cp(col(6), c("s1", 1, 2))
    ts(col(10), c("ki"), 16.0, A.mult)
    ts(c("s1", 0, 1), c("ip"), 16, A.bitwise_and)
    ts(col(8), c("s1", 0, 1), 1.0 / 16, A.mult)
    ts(col(7), col(8), -1.0, A.mult, 1.0, A.add)
    ts(c("keq"), c("c16"), col(1), A.is_equal)
    tt(col(9), c("keq", 0, 1), c("keq", 1, 2), A.add)
    ts(c("e0"), c("ci", 0, 160), col(3), A.is_equal, col(7), A.mult)
    ts(c("e1"), c("ci", 0, 160), col(3), A.is_equal, col(8), A.mult)

    def swap16(psname):
        for de in range(2):
            ts(c("rt", 128 * de, 128 * de + 128), pr("tr", de), -2048.0, A.add)
        for al in range(2):
            o = c(psname, 128 * al, 128 * al + 128)
            mms([(o, c("e%d" % al, 16 + 16 * (al - de), 144 + 16 * (al - de)), c("rt", 128 * de, 128 * de + 128), de == 0, de == 1)
                 for de in range(2)], o)
        for al in range(2):
            ts(pr("tr", al), c(psname, 128 * al, 128 * al + 128), 2048.0, A.add)

    def flip(a):
        return (T.tr[:, a, :], "tr", 32 * a, 32 * a + 32)

    def conv_in(src, psname):
        for a in range(8):
            i, o = c(src, 32 * a, 32 * a + 32), flip(a)
            run("v", [i], [o], lambda v, i=i, o=o: v.transpose(o[0], i[0]))
        swap16(psname)

    def conv_out(dst, psname):
        swap16(psname)
        for a in range(8):
            o, i = c(dst, 32 * a, 32 * a + 32), flip(a)
            run("v", [i], [o], lambda v, i=i, o=o: v.transpose(o[0], i[0]))

    for q in range(16):
        cp(c("tf", 16 * q, 16 * q + 16), c("roc", q, 256, 16))
    conv_in("tf", "p1")
    cp(c("of"), c("tr"))
    ts(c("tg"), c("of"), 256.0, A.is_lt)
    ts(c("of"), c("of"), 1.0, A.add)
    tt(c("oi"), c("of"), c("tg"), A.mult)
    ts(c("p6", 0, 256), c("ci"), col(4), A.add)
    ts(c("hv"), c("c16"), 2.0, A.mult, col(5), A.add)
    ts(c("zs"), c("ci", 0, 144), col(2), A.is_equal)
    ts(c("zn"), c("zs"), -1.0, A.mult)
    ts(c("idb"), c("ci", 0, 128), col(0), A.is_equal)
    ts(c("idn"), c("idb"), -1.0, A.mult)

    def q_lists():
        cp(c("qu"), c("qi"))

    def more_constants():
        ts(c("za"), c("ci", 0, 144), col(2), A.is_equal, col(9), A.mult)
        ts(c("zf"), c("ci", 0, 144), col(2), A.is_equal, c("keq", 2, 3), A.mult)
        ts(c("zw"), c("ci", 0, 144), col(2), A.is_equal, col(10), A.mult)
        o = c("p5", 0, 16)
        mms([(o, c("zw", 15 - i, 143 - i), c("ww", 1 + i, 257, 16), i == 0, i == 15) for i in range(16)], o)
        ts(c("ws"), o, 2040.0, A.add)
        for n in ("mw", "lw", "a16", "a17"):
            fill(c(n), 0.0)
        ts(c("cw", 4096, 4097), c("keq", 0, 1), NOB, A.mult)
        ts(c("mw", 0, 1), c("keq", 0, 1), 16384.0, A.mult)
        ts(c("bo"), c("um", 0, 128), col(6), A.is_equal)
        for r in range(16):
            ts(c("br", 128 * r, 128 * r + 128), c("bo"), c("keq", r, r + 1), A.mult)
        ts(c("ni"), c("ci"), col(4), A.add)
        ts(c("na"), c("ni"), 127, A.bitwise_and)
        cp(col(11), c("rth"))
        for t in range(RO):
            x = c("thl", 256 * t, 256 * t + 256)
            ts(x, c("na"), float(16 * t), A.is_equal, -30000.0, A.mult)
            act(x, x, F.Identity, bias=col(11), scale=1.0)
        ts(c("rr"), c("jl"), 16.0, A.is_lt)
        ts(c("uo"), c("c16"), 16.0, A.mult, col(1), A.add)
        ts(c("pll"), c("uo"), 256.0, A.add)
        ts(c("lt"), c("lt"), col(1), A.is_le, 2048.0, A.mult)
        ts(c("ko"), c("jl"), -8192.0, A.mult, 131072.0, A.add)
        cp(c("tf"), c("rqs"))
        conv_in("tf", "p5")
        cp(c("qi"), c("tr"))
        q_lists()

    def bc16(out, src, buf):
        cp(c(buf, 0, 256, 16), src)
        scan(out, c("rr"), c(buf))

    def q_update():
        oh, q2 = c("tk", 0, 256), c("tk", 256, 512)
        tt(q2, c("qd"), c("p5", 0, 256), A.add)
        ts(q2, q2, 4096.0, A.min)
        ts(c("sl", 0, 16), c("p5", 256, 272), 0.0, A.is_gt)
        tt(c("sl", 0, 16), c("sl", 0, 16), c("wi"), A.mult)
        tt(c("sl", 0, 16), c("sl", 0, 16), c("f16"), A.mult)
        ts(c("sl", 16, 32), c("ui"), 16.0, A.mult, 16.0 - 4096.0, A.add)
        tt(c("sl", 16, 32), c("sl", 16, 32), c("p5", 256, 272), A.subtract)
        rep = c("p6", 256, 512)
        bc16(rep, c("sl", 0, 16), "a16")
        tt(oh, c("jl"), rep, A.is_equal)
        bc16(rep, c("sl", 16, 32), "a17")
        tt(c("p7", 0, 256), oh, rep, A.mult)
        tt(c("qi"), q2, c("p7", 0, 256), A.add)

    def x_lists():
        for a in (0, 128):
            act(c("lvb", a, a + 128), c("lv", a, a + 128), F.Copy, scale=4608.0)
        tt(c("xl"), c("lvb"), c("p6", 256, 512), A.subtract)
        dma("y", lane("xw", 0, 4096), c("xl"), "dxl")
        cp(c("le32"), c("p6", 256 + 15, 512, 16))
        act(c("le"), c("le32"))
        dma("y", lane("lw", 0, 256), c("le"), "dle")

    def x_gather(q, k):
        gat(q, c("xg", 1024 * k, 1024 * k + 1024), c("xw"), c("qdu", 64 * k, 64 * k + 64))

    def x_ext(k):
        ext(c("p5", 64 * k, 64 * k + 64), "za", "xg", 64 * k, 64)

    def len_gather():
        gat("s", c("lg"), c("lw"), c("uu"))

    def len_ext():
        ext(c("p5", 256, 272), "za", "lg", 0, 16)

    for t in range(RO):
        cp(c("ou"), c("oi"))
        boost[0] = BOOST[0]
        for k in range(4):
            gat("s", c("wg", 1024 * k, 1024 * k + 1024), c("ww"), c("ou", 64 * k, 64 * k + 64))
        boost[0] = 0.0
        ts(c("a2", 1, 256), c("ou", 0, 255), 2.0, A.mult, -1.0, A.add)
        cp(c("a2", 0, 256, 16), c("hv"))
        tt(c("t1"), c("a2"), c("p6", 0, 256), A.mult)
        ts(c("t2"), c("t1"), 4, A.arith_shift_right)
        tt(c("p7", 0, 256), c("t2"), c("p6", 0, 256), A.add)
        boost[0] = BOOST[4]
        act(c("p37"), c("oi"), F.Identity, scale=37.0, bias=77.0 * t - 37.0)
        boost[0] = 0.0
        tt(c("hi", 0, 256), c("p37"), c("p7", 0, 256), A.add)
        tt(pr("hi", 0, 8), pr("p37", 0), pr("p7", 1), A.add)
        tt(pr("hi", 1, 8), pr("p37", 1), pr("p7", 0), A.add)
        ts(c("hj"), c("hi"), 4095, A.bitwise_and)
        cp(c("hu"), c("hj"))
        for par in range(2):
            act(c("em", 128 * par, 128 * par + 128), pr("oi", par), F.Relu, scale=-16384.0, bias=16384.0)
        o = c("p3", 0, 128)
        mms([(o, c("idb"), c("em", 128 * par, 128 * par + 128), par == 0, par == 1) for par in range(2)], o)
        for (s, a, n, via) in PIECES:
            w, h = c("wg", 16 * a, 16 * a + 16 * n), c("hu", 256 * s + a, 256 * s + a + n)
            m = c("mn", 4096 * s + 16 * a, 4096 * s + 16 * a + 16 * n)
            o = c("p%d" % s, a, a + n)
            if not via:
                run("v", [c("xs"), h, w], [m], lambda v, h=h, w=w, m=m: v.tensor_tensor(m[0], T.xs[:, 0:4096].indirect(h[0]), w[0], A.min),
                    60 + GATHER * 16 * n)
                ext(o, "zs", "mn", 256 * s + a, n)
                continue
            x = c("xo", 0, 16 * n)
            boost[0] = BOOST[7]
            gat("s", x, c("xs"), h)
            for j in range(n // 32):
                d = c(("p2", "p4")[j], 0, 512)
                mms([(d, c("idb"), w[5](512 * j, 512 * j + 512), True, False), (d, c("idn"), x[5](512 * j, 512 * j + 512), False, True)], d)
                act(m[5](512 * j, 512 * j + 512), d, F.Relu)
            items = [(o, c("zs", 15 - i, 143 - i), c("wg", 16 * a + i, 16 * (a + n), 16), i == 0, False) for i in range(16)]
            b = 4096 * s + 16 * a
            mms(items + [(o, c("zn", 15 - i, 143 - i), c("mn", b + i, b + 16 * n, 16), False, i == 15) for i in range(16)], o)
            boost[0] = 0.0
        act(c("m1s"), c("p0", 0, 256))
        act(c("m1o"), c("m1s"), F.Identity, bias=-2040.0, scale=1.0)
        if t == 0:
            more_constants()
        tt(c("p7", 256, 512), c("p1", 0, 256), c("m1s"), A.subtract)
        cp(c("dob"), pr("p7", 1, 8))
        tt(c("ds"), pr("p7", 0, 8), c("dob"), A.add)
        for par in range(2):
            tt(pr("sw", par), c("ds"), c("p3", 0, 128), A.is_gt)
        for par in range(2):
            ts(pr("swd", par), pr("sw", par), 16.0 - 32.0 * par, A.mult)
        dma("y", lane("cw", 2, 4096), c("swd"), "dsw")
        tt(c("p7", 0, 256), c("p7", 256, 512), c("sw"), A.mult)
        tt(c("p7", 256, 512), c("p7", 0, 256), c("m1o"), A.add)
        cp(c("chi"), c("p7", 256, 512))
        dma("y", lane("cw", 0, 4096), c("chi"), "dhi")
        tt(c("clo"), c("p7", 256, 512), c("chi"), A.subtract)
        dma("s", lane("cw", 1, 4096), c("clo"), "dlo")
        if t:
            q_update()
            q_lists()
        for k in (0, 2, 1, 3):
            gat("v" if k < 2 else "s", c("cg", 1024 * k, 1024 * k + 1024), c("cw"), c("qu", 64 * k, 64 * k + 64))
            bank = ("p4", "p5", "p1", "p0")[k]
            ext(c(bank, 0, 64), "za", "cg", 64 * k, 64)
            for j in range(4):
                i, o = c(bank, 16 * j, 16 * j + 16), c("bs", 16 * t + 4 * k + j, 16 * t + 4 * k + j + 1)
                i2 = T.p0[:, j, :] if bank == "p0" else i[0]
                run("v", [i], [o], lambda v, i2=i2, o=o: v.tensor_reduce(o[0], i2, AxisListType.X, A.max))
            act(c("cs", 64 * k, 64 * k + 64), c(bank, 0, 64), F.Identity, bias=col(11), scale=1.0)
        ext(c("p3", 256, 512), "zf", "cg", 0, 256)
        mine = c("bs", 16 * t, 16 * t + 16)
        others = [d for d in T.cores if d != core]
        mask = 0xFFFFFFFF
        for d in others:
            mask &= topo.mask(core, d)
        eng = bin(mask).count("1")
        ids = []
        for d in others:
            rid, pid, _ = topo.addr(d)
            ids.append(DstId(rid=rid, pnc=pid))
        here = 64 * t + 16 * rank
        send = RemoteDMATransfer(dst_ids=ids, dma_engine_mask=mask, remote_sem=T.sem["arr%d" % t], srcs=[mine[0]],
                                 dsts=[T.land[:, here:here + 16] for d in others])
        wire = (None, "wire", t, t + 1)
        add("g", [mine], [wire], lambda e, s, send=send: e.remote_dma_fused([send], local_sem=s), 0.5, "snt", eng, 0.0)
        add("n", [], [c("land", 64 * t, 64 * t + 64), wire], None, 0.0, "arr%d" % t, eng * (n_ranks - 1), 4.0)
        fill(c("qw"), 0.0)
        tt(c("p7", 0, 128), pr("oi", 1), pr("oi", 0), A.subtract)
        tt(c("p7", 128, 256), c("p7", 0, 128), pr("sw", 0), A.mult)
        tt(pr("o2", 0), c("p7", 128, 256), pr("oi", 0), A.add)
        tt(pr("o2", 1), pr("oi", 1), c("p7", 128, 256), A.subtract)
        cp(c("ou2"), c("o2"))
        cp(c("ccs"), c("p7", 256, 512))
        tt(c("p7", 0, 128), pr("p7", 1, 8), pr("ccs", 0), A.subtract)
        tt(c("p7", 128, 256), c("p7", 0, 128), pr("sw", 0), A.mult)
        tt(c("e1l"), c("ccs"), c("thl", 256 * t, 256 * t + 256), A.add)
        tt(pr("c2l", 0), c("p7", 128, 256), pr("e1l", 0), A.add)
        tt(pr("c2l", 1), pr("e1l", 1), c("p7", 128, 256), A.subtract)
        ts(c("g32"), c("o2"), 16.0, A.mult)
        tt(c("g32"), c("g32"), c("ko"), A.add)
        tt(c("qd"), c("p3", 256, 512), c("qi"), A.add)
        cp(c("qdu"), c("qd"))
        ts(c("hq"), c("qd"), 4096 + 127, A.bitwise_and)
        ts(c("p7", 0, 256), c("hq"), float(16 * t), A.is_equal, -30000.0, A.mult)
        tt(c("cx"), c("p7", 0, 256), c("cs"), A.add)
        lands = [c("land", 64 * t + 16 * r, 64 * t + 16 * r + 16) for r in range(n_ranks)]
        lower, higher = lands[:rank], lands[rank + 1:]
        seq = lower + higher
        boost[0] = BOOST[2]
        m2 = [c("ap", 0, 16), c("ap", 16, 32)]
        tt(m2[0], mine, seq[0], A.max)
        tt(m2[1], seq[1], seq[2], A.max)
        tt(c("m16"), m2[0], m2[1], A.max)
        tt(c("mm"), m2[0], m2[1], A.max)
        mms([(c("p4", r, 256, 16), c("br", 128 * r, 128 * r + 128), c("m16"), True, True) for r in range(16)], c("p4", 0, 256))
        ts(c("mt"), c("p4", 0, 256), c("keq", 1, 2), A.mult)
        tt(c("mw", 1, 257), c("p4", 0, 256), c("mt"), A.subtract)
        boost[0] = 0.0
        for (q, a, n) in MPIECES:
            if q == "s":
                gat("s", c("mg", 16 * a, 16 * a + 16 * n), c("mw"), c("ou2", a, a + n))
        tt(c("s1"), c("mm"), c("ws"), A.add)
        ts(c("ui"), c("s1"), 255, A.bitwise_and)
        bc16(c("p6", 256, 512), c("mm"), "a16")
        tt(c("p7", 256, 512), c("p6", 256, 512), c("cx"), A.is_gt)
        tt(c("jv"), c("p7", 256, 512), c("jl"), A.mult)
        tt(c("t8"), k3("jv", 0, 8), k3("jv", 8, 16), A.max)
        tt(c("t4"), k3("t8", 0, 4), k3("t8", 4, 8), A.max)
        tt(c("t2x"), k3("t4", 0, 2), k3("t4", 2, 4), A.max)
        tt(c("f16"), k1("t2x", 0), k1("t2x", 1), A.max)
        ts(c("va"), c("f16"), 0.0, A.is_gt)
        h1, h2, lm = c("sl", 32, 48), c("sl", 48, 64), c("ap", 48, 64)
        tt(h1, mine, c("mm"), A.is_equal)
        if lower:
            top = lower[0]
            for x in lower[1:]:
                tt(lm, top, x, A.max)
                top = lm
            tt(h2, top, c("mm"), A.is_lt)
            tt(h1, h1, h2, A.mult)
        tt(c("va"), c("va"), h1, A.mult)
        ts(c("vb"), c("ui"), -1024.0, A.add)
        tt(c("vb"), c("vb"), c("va"), A.mult)
        ts(c("uh"), c("vb"), 1024.0, A.add)
        ts(c("uc"), c("vb"), 1024.0, A.add)
        mms([(c("p3", r, 256, 16), c("br", 128 * r, 128 * r + 128), c("uh"), True, True) for r in range(16)], c("p3", 0, 256))
        cp(c("uu"), c("ui"))
        cp(c("ub"), c("p3", 0, 256))
        tt(c("um"), c("p3", 0, 256), c("lt"), A.add)
        bc16(c("p6", 256, 512), c("uc"), "a16")
        tt(c("eqb", 1920, 2176), c("um"), c("p6", 256, 512), A.is_equal)
        at, los = [], [(c("p1", 0, 256), c("bo"), c("eqb", 1920, 2176))]
        for pc in range(15):
            a = sum(240 - 16 * z for z in range(pc))
            o = c("eqb", a, a + 240 - 16 * pc)
            ts(o, c("ub", 16 * pc + 16, 256), c("uc", pc, pc + 1), A.is_equal)
            los.append((c("p1", 16 * pc + 16, 256), c("bo"), o))
        for a, b in ((0, 6), (6, 11), (11, 16)):
            mms([(los[z] + (z == 0, z == 15)) for z in range(a, b)], c("p1", 0, 256))
        ts(c("lz"), c("p1", 0, 256), 0.0, A.is_equal)
        ext(c("p1", 272, 288), "zf", "lz", 0, 16)
        tt(c("wi"), c("va"), c("p1", 272, 288), A.mult)
        tt(c("uo"), c("uc"), c("pll"), A.subtract)
        tt(c("uo"), c("uo"), c("wi"), A.mult)
        tt(c("uo"), c("uo"), c("pll"), A.add)
        cp(c("uou"), c("uo"))
        run("v", [c("pv"), c("uou")], [c("qw")], lambda v: v.tensor_copy(T.qw[:, 0:512].indirect(T.uou[:, 0:16]), T.pv[:, 0:256]), 900)
        o = c("p1", 288, 304)
        mms([(o, c("zf", 15 - r, 143 - r), c("qw", 16 * r, 16 * r + 16), r == 0, r == 15) for r in range(16)], o)
        for (q, a, n) in MPIECES:
            if q == "v":
                gat("v", c("mg", 16 * a, 16 * a + 16 * n), c("mw"), c("ou2", a, a + n))
            ext(c("p4", a, a + n), "za", "mg", a, n)
        sh = c("p6", 256, 512)
        boost[0] = BOOST[5]
        tt(c("lv"), c("p4", 0, 256), c("c2l"), A.is_gt)
        boost[0] = BOOST[6]
        for a in (0, 128):
            act(c("st", a, a + 128), c("lv", a, a + 128), F.Identity, scale=-1.0, bias=1.0)
        boost[0] = BOOST[5]
        scan(sh, c("rr"), c("lv"))
        boost[0] = 0.0
        tt(c("p7", 256, 512), c("g32"), sh, A.add)
        tt(c("yb"), c("p7", 256, 512), c("st"), A.mult)
        boost[0] = BOOST[1]
        x_lists()
        boost[0] = 0.0
        bc16(sh, c("le32"), "a17")
        tt(c("fe"), c("jl"), sh, A.is_equal)
        tt(c("p7", 256, 512), c("jl"), sh, A.is_gt)
        for b in range(4):
            d = 1 << b
            y, m, to = k3("yb", d, 16), k3("p2", d, 16), k3("yb", 0, 16 - d)
            ts(k3("tb", d, 16), y, b, A.arith_shift_right, 1, A.bitwise_and)
            tt(m, k3("tb", d, 16), y, A.mult)
            tt(to, to, m, A.max)
        ts(c("yb"), c("yb"), 4, A.arith_shift_right, 511, A.bitwise_and)
        tt(c("yb"), c("yb"), c("p7", 256, 512), A.mult)
        bc16(sh, c("p1", 288, 304), "a16")
        tt(c("p7", 0, 256), c("fe"), sh, A.mult)
        tt(c("oi"), c("yb"), c("p7", 0, 256), A.add)
        boost[0] = BOOST[3]
        for k in range(4):
            x_gather("v" if t == RO - 1 and k == 3 else "s", k)
            x_ext(k)
        len_gather()
        len_ext()
        boost[0] = 0.0
    act(c("tf"), c("oi"), F.Relu, scale=-257.0, bias=257.0)
    act(c("tg"), c("oi"), F.Identity, scale=1.0, bias=-1.0)
    tt(c("tr"), c("tf"), c("tg"), A.add)
    conv_out("of", "p1")
    for q in range(16):
        act(c("um", q, 256, 16), c("of", 16 * q, 16 * q + 16))
    dma("y", T.yoc[:, :], c("um"), "dyo")
    q_update()
    cp(c("tr"), c("qi"))
    conv_out("tg", "p1")
    dma("y", T.yq[:, :], c("tg"), "dyq")
    for i in schedule():
        q, rd, wr, call, hold, sem, inc = ops[i][:7]
        if call is None:
            cnt[sem] += inc
            note(q, [], wr[:1], sem, cnt[sem])
            continue
        order(q, rd, wr)
        cnt[sem] += inc
        call(queues[q], T.sem[sem])
        note(q, rd, wr, sem, cnt[sem])
    for s in SEMAPHORES:
        if cnt[s] > known["g"].get(s, 0):
            g.wait_ge(T.sem[s], cnt[s])
